import numpy as np
import ml_dtypes


def mxq(x, axis, fmt="e4m3"):
    dtype, down = {"e4m3": (ml_dtypes.float8_e4m3fn, 7), "e5m2": (ml_dtypes.float8_e5m2, 14)}[fmt]
    v = np.moveaxis(np.asarray(x, np.float32).astype(ml_dtypes.bfloat16).astype(np.float64), axis, -1)
    blocks = v.reshape(v.shape[:-1] + (-1, 32))
    amax = np.abs(blocks).max(-1, keepdims=True)
    byte = np.maximum(np.where(amax > 0, np.frexp(amax)[1] - 1 + 127, 0) - down, 1)
    scale = np.exp2(byte - 127.0)
    codes = (blocks / scale).astype(np.float32).astype(dtype).astype(np.float64)
    return np.moveaxis((codes * scale).reshape(v.shape), -1, axis)


WIDE = False


def mx_kscale(k):
    if not WIDE:
        return np.ones(k)
    levels = np.array([10, -10, 5, -5, 0])
    if k % 512:
        return np.exp2(np.random.permutation(np.resize(levels, k // 32))).repeat(32)
    a = np.empty((k // 512, 16))
    for p in range(k // 512):
        a[p, :8] = np.random.permutation(np.resize(levels, 8))
        for g in range(8):
            far = levels[np.abs(levels - a[p, g]) >= 10]
            a[p, g + 8] = far[np.random.randint(len(far))]
    return np.exp2(a.ravel()).repeat(32)


BF16 = ml_dtypes.bfloat16


def bf(x):
    return np.asarray(x, np.float32).astype(BF16)


def f64(x):
    return np.asarray(x).astype(np.float64)

def planes(Y):
    n, m = Y.shape
    b = f64(bf(Y)).reshape(n // 32, 32, m)
    amax = np.abs(b).max(1)
    byte = np.clip(np.where(amax > 0, np.frexp(amax)[1] - 1 + 127 - 7, 1), 1, 254)
    codes = (b * np.exp2(127.0 - byte)[:, None, :]).reshape(n, m).astype(np.float32).astype(ml_dtypes.float8_e4m3fn).view(np.uint8)
    words = codes.reshape(n // 512, 128, 4, m).transpose(0, 1, 3, 2)
    return np.ascontiguousarray(words), np.ascontiguousarray(byte.astype(np.uint8).reshape(n // 512, 16, m))


M, R, Z, U = 1024, 1024, 1024, 1024


def log_elasticity(a, s):
    return a * 2.0 / (1.0 + s * s)[None, :]


def setup_inputs():
    r, t, u = mx_kscale(R), mx_kscale(M), mx_kscale(U)
    n = bf(np.random.standard_normal((M, R)) / np.sqrt(R) * r[None, :])
    v = bf(np.random.uniform(0.5, 1.5, R))
    a = bf(np.random.standard_normal((R, M)) / r[:, None] * t[None, :])
    s = bf(np.random.uniform(0.5, 1.5, M))
    c = bf(np.random.standard_normal((M, Z)) / np.sqrt(M) / t[:, None])
    l = bf(np.random.standard_normal((M, U)) / np.sqrt(U) * u[None, :])
    cu = bf(np.random.standard_normal((U, Z)) / u[:, None])
    return {"n": n, "v": v, "a": a, "s": s, "c": c, "l": l, "cu": cu}


def core(n, v, a, s, c, l, cu):
    n, v, a, s = f64(n), f64(v), f64(a), f64(s)
    eps = log_elasticity(a, s)
    nv = n * v[None, :]
    k = mxq(nv, 1, "e4m3") @ mxq(eps, 0, "e4m3")
    jac = k / s[:, None]
    p = mxq(jac, 1, "e4m3") @ mxq(f64(c), 0, "e4m3")
    f = mxq(f64(l), 1, "e4m3") @ mxq(f64(cu), 0, "e4m3")
    return p + f


def reference(n, v, a, s, c, l, cu):
    R_out = core(n, v, a, s, c, l, cu)
    words, scales = planes(R_out.T)
    return R_out, words, scales

@@ -1,0 +1,501 @@
+from contextlib import ExitStack
+
+import concourse.mybir as mybir
+from concourse.masks import make_identity
+
+D = 1024
+FLOPS = 3 * 2 * D * D * D
+
+F32 = mybir.dt.float32
+BF16 = mybir.dt.bfloat16
+U32 = mybir.dt.uint32
+I32 = mybir.dt.int32
+U8 = mybir.dt.uint8
+FP8X4 = mybir.dt.float8_e4m3fn_x4
+MULT = mybir.AluOpType.mult
+ADD = mybir.AluOpType.add
+
+P = 128
+SB = 4
+ROWS = 256
+TRB = 2
+
+
+def tile_relativefluctuationcovariancedrift_kernel(tc, n, v, a, s, c, l, cu, out_0, out_1, out_2):
+    nc = tc.nc
+    with ExitStack() as ctx:
+        keep = ctx.enter_context(tc.tile_pool(name="keep", bufs=1))
+        work = ctx.enter_context(tc.tile_pool(name="work", bufs=2))
+        psum = ctx.enter_context(tc.psum_pool(name="psum", bufs=1))
+        ctx.enter_context(tc.manual_schedule())
+
+        def kt(name, shape, dtype):
+            return keep.tile(shape, dtype, name=name, tag=name, align_bytes=64)
+
+        def wt(tag, shape, dtype, bufs):
+            return work.tile(shape, dtype, name=tag, tag=tag, bufs=bufs, align_bytes=64)
+
+        def bank(tag, shape, dtype, bufs):
+            return psum.tile(shape, dtype, name=tag, tag=tag, bufs=bufs)
+
+        srow = kt("srow", [P, P], BF16)
+        nc.vector.memset(srow[:], 0.0)
+        ident = kt("ident", [P, P], F32)
+        make_identity(nc, ident[:])
+        identb = kt("identb", [P, P], BF16)
+        nc.vector.tensor_copy(out=identb[:], in_=ident[:])
+
+        for g in range(2):
+            nc.sync.dma_start(
+                out=srow[4 * g : 4 * g + 4, :].rearrange("t (b q) -> t b q", q=8),
+                in_=s[512 * g : 512 * g + 512].rearrange("(b t q) -> t b q", t=4, q=8),
+            )
+        nc.sync.dma_start(out=srow[8:16, :], in_=s.rearrange("(x p) -> x p", p=P))
+        v4 = kt("v4", [P, 2, 4], BF16)
+        nc.sync.dma_start(out=v4[:], in_=v.rearrange("(g p j) -> p g j", p=P, j=4))
+
+        n_raw, l_raw = [], []
+        for k in range(SB):
+            n_raw.append(kt("n_raw%d" % k, [P, 2, D], BF16))
+            l_raw.append(kt("l_raw%d" % k, [P, 2, D], BF16))
+        a_raw = {}
+        cu_raw = {}
+        for g in range(2):
+            for h in range(2):
+                a_raw[g, h] = kt("a_raw%d%d" % (g, h), [P, 4, 512], BF16)
+                cu_raw[g, h] = kt("cu_raw%d%d" % (g, h), [P, 4, 512], BF16)
+        c_raw = {(g, h): kt("c_raw%d%d" % (g, h), [P, 4, 512], BF16) for g in range(2) for h in range(2)}
+
+        def load_n(k):
+            nc.sync.dma_start(out=n_raw[k][:], in_=n[ROWS * k : ROWS * k + ROWS, :].rearrange("(b p) r -> p b r", p=P))
+
+        def load_l(k):
+            nc.sync.dma_start(out=l_raw[k][:], in_=l[ROWS * k : ROWS * k + ROWS, :].rearrange("(b p) r -> p b r", p=P))
+
+        def load_part(raw, src, g, h):
+            nc.sync.dma_start(
+                out=raw[g, h][:],
+                in_=src[512 * g : 512 * g + 512, 512 * h : 512 * h + 512].rearrange("(p j) w -> p j w", j=4),
+            )
+
+        def load_c(g, h):
+            rows = c[512 * g : 512 * g + 512, 512 * h : 512 * h + 512].rearrange("(b t q) z -> t b q z", t=4, q=8)
+            for t in range(4):
+                nc.sync.dma_start(out=c_raw[g, h][:, t, :], in_=rows[t])
+
+        load_part(a_raw, a, 0, 0)
+        load_part(cu_raw, cu, 0, 0)
+        load_n(0)
+        load_part(a_raw, a, 1, 0)
+        load_part(a_raw, a, 1, 1)
+        load_l(0)
+        load_part(cu_raw, cu, 1, 0)
+        load_part(a_raw, a, 0, 1)
+        load_c(0, 0)
+        load_c(1, 0)
+        load_n(1)
+        load_c(0, 1)
+        load_part(cu_raw, cu, 0, 1)
+        load_c(1, 1)
+        load_part(cu_raw, cu, 1, 1)
+        load_l(1)
+        load_n(2)
+        load_l(2)
+        load_n(3)
+        load_l(3)
+
+        s_ps = bank("tr", [P, P], BF16, TRB)
+        nc.tensor.transpose(s_ps[:], srow[:], identb[:])
+        s_cols = kt("s_cols", [P, 16], F32)
+        nc.vector.tensor_copy(out=s_cols[:], in_=s_ps[:, 0:16])
+        s_sq = kt("s_sq", [P, 8], F32)
+        nc.vector.tensor_tensor(out=s_sq[:], in0=s_cols[:, 0:8], in1=s_cols[:, 0:8], op=MULT)
+        s_half = kt("s_half", [P, 8], F32)
+        nc.vector.tensor_scalar(out=s_half[:], in0=s_sq[:], scalar1=0.5, scalar2=0.5, op0=MULT, op1=ADD)
+        e4 = kt("e4", [P, 8], F32)
+        nc.vector.reciprocal(out=e4[:], in_=s_half[:])
+        rs8 = kt("rs8", [P, 8], F32)
+        nc.vector.reciprocal(out=rs8[:], in_=s_cols[:, 8:16])
+
+        e_ps = {}
+
+        def spread_e(G):
+            e_ps[G] = bank("s2", [P, 4, P], F32, 4)
+            for t in range(4):
+                j = 4 * G + t
+                nc.tensor.transpose(e_ps[G][:, t, :], e4[:, j : j + 1].to_broadcast([P, P]), ident[:])
+
+        rs_row = kt("rs_row", [P, D], F32)
+
+        def spread_rs(y):
+            b = bank("s1", [P, 4, P], F32, 2)
+            for x in range(4):
+                nc.tensor.transpose(b[:, x, :], rs8[:, 4 * y + x : 4 * y + x + 1].to_broadcast([P, P]), ident[:])
+            nc.scalar.copy(out=rs_row[:, 512 * y : 512 * y + 512], in_=b[:].rearrange("p x i -> p (x i)"))
+
+        tr_ps = {}
+
+        def turn(key, words, g):
+            b = bank("tr", [P, 2, 2, P], F32, TRB)
+            for u in range(2):
+                for ib in range(2):
+                    nc.tensor.transpose(b[:, u, ib, :], words[:, ib, 256 * g + u : 256 * g + 256 : 2], ident[:])
+            tr_ps[key] = b
+
+        def turn_n(k, g):
+            turn(("n", k, g), n_raw[k][:].bitcast(F32), g)
+
+        def turn_l(k, g):
+            turn(("l", k, g), l_raw[k][:].bitcast(F32), g)
+
+        nv_bf, n_codes, n_scales = {}, {}, {}
+        l_bf, l_codes, l_scales = {}, {}, {}
+
+        def mul_v(k, g):
+            if g == 0:
+                nv_bf[k] = wt("nv_bf", [P, 2, ROWS, 4], BF16, 2)
+            b = tr_ps.pop(("n", k, g))
+            nc.vector.tensor_tensor(
+                out=nv_bf[k][:, g].rearrange("p i (u e) -> p i u e", u=2),
+                in0=b[:].rearrange("p u b i -> p (u b i)").bitcast(BF16).rearrange("p (u i e) -> p i u e", u=2, e=2),
+                in1=v4[:, g].rearrange("p (u e) -> p u e", u=2).unsqueeze(1).to_broadcast([P, ROWS, 2, 2]),
+                op=MULT,
+            )
+
+        def quant_n(k):
+            n_codes[k] = kt("n_codes%d" % k, [P, 2, ROWS], U32)
+            n_scales[k] = kt("n_scales%d" % k, [P, 2, ROWS], U8)
+            nc.vector.quantize_mx(
+                out=n_codes[k][:].rearrange("p g i -> p (g i)").bitcast(FP8X4),
+                scales=n_scales[k][:].rearrange("p g i -> p (g i)"),
+                in_=nv_bf[k][:].rearrange("p g i t -> p (g i t)"),
+            )
+
+        def out_l(k, g):
+            if g == 0:
+                l_bf[k] = wt("l_bf", [P, 2, ROWS, 4], BF16, 3)
+            b = tr_ps.pop(("l", k, g))
+            nc.scalar.copy(
+                out=l_bf[k][:, g].rearrange("p i t -> p (i t)").bitcast(F32).rearrange("p (i u) -> p i u", u=2),
+                in_=b[:].rearrange("p u b i -> p (b i) u"),
+            )
+
+        def quant_l(k):
+            l_codes[k] = kt("l_codes%d" % k, [P, 2, ROWS], U32)
+            l_scales[k] = kt("l_scales%d" % k, [P, 2, ROWS], U8)
+            nc.vector.quantize_mx(
+                out=l_codes[k][:].rearrange("p g i -> p (g i)").bitcast(FP8X4),
+                scales=l_scales[k][:].rearrange("p g i -> p (g i)"),
+                in_=l_bf[k][:].rearrange("p g i t -> p (g i t)"),
+            )
+
+        eps_bf, eps_codes, eps_scales = {}, {}, {}
+
+        e_row = kt("e_row", [P, 4, P], F32)
+
+        def keep_e(G):
+            nc.scalar.copy(out=e_row[:].rearrange("p t m -> p (t m)"), in_=e_ps[G][:].rearrange("p t m -> p (t m)"))
+
+        def mul_e(g, G, ts, on_gpsimd=False):
+            if (g, G) not in eps_bf:
+                eps_bf[g, G] = wt("eps_bf", [P, 4, P, 4], BF16, 3)
+            for t in ts:
+                e_t = e_row[:, t] if on_gpsimd else e_ps[G][:, t]
+                (nc.gpsimd if on_gpsimd else nc.vector).tensor_tensor(
+                    out=eps_bf[g, G][:, t].rearrange("p (b q) j -> p b q j", q=8),
+                    in0=a_raw[g, G][:].rearrange("p j (b t q) -> p t b q j", t=4, q=8)[:, t],
+                    in1=e_t.rearrange("p (b q) -> p b q", q=8).unsqueeze(3).to_broadcast([P, 16, 8, 4]),
+                    op=MULT,
+                )
+
+        def quant_e(g, G):
+            eps_codes[g, G] = kt("eps_codes%d%d" % (g, G), [P, 512], U32)
+            eps_scales[g, G] = kt("eps_scales%d%d" % (g, G), [P, 512], U8)
+            nc.vector.quantize_mx(
+                out=eps_codes[g, G][:].bitcast(FP8X4),
+                scales=eps_scales[g, G][:],
+                in_=eps_bf[g, G][:].rearrange("p t m j -> p (t m j)"),
+            )
+
+        w_bf, w_codes, w_scales = {}, {}, {}
+
+        def inter(mat, g, h, engine):
+            dst = wt("w_bf", [P, 512, 4], BF16, 6)
+            w_bf[mat, g, h] = dst
+            src = cu_raw[g, h][:] if mat == "cu" else c_raw[g, h][:]
+            if engine == "s":
+                nc.scalar.copy(
+                    out=dst[:].rearrange("p (x i) j -> p x j i", i=4),
+                    in_=src.rearrange("p j (x i) -> p x j i", i=4),
+                )
+            elif engine == "v":
+                nc.vector.tensor_copy(
+                    out=dst[:].rearrange("p (x i) j -> p x j i", i=4),
+                    in_=src.rearrange("p j (x i) -> p x j i", i=4),
+                )
+            else:
+                for y in range(4):
+                    nc.gpsimd.tensor_scalar(
+                        out=dst[:, 128 * y : 128 * y + 128, :],
+                        in0=src.rearrange("p j z -> p z j")[:, 128 * y : 128 * y + 128, :],
+                        scalar1=1.0,
+                        scalar2=0.0,
+                        op0=MULT,
+                        op1=ADD,
+                    )
+
+        def quant_w(mat, g, h):
+            key = (mat, g, h)
+            w_codes[key] = kt("%s_codes%d%d" % key, [P, 512], U32)
+            w_scales[key] = kt("%s_scales%d%d" % key, [P, 512], U8)
+            nc.vector.quantize_mx(
+                out=w_codes[key][:].bitcast(FP8X4),
+                scales=w_scales[key][:],
+                in_=w_bf[key][:].rearrange("p z j -> p (z j)"),
+            )
+
+        k_ps, jac_bf, j_codes, j_scales = {}, {}, {}, {}
+
+        def stage1(k, ib, G):
+            b = bank("s1", [P, 4, P], F32, 2)
+            cols = slice(P * ib, P * ib + P)
+            for t in range(4):
+                for g in range(2):
+                    nc.tensor.matmul_mx(
+                        out=b[:, t, :],
+                        lhsT=eps_codes[g, G][:, P * t : P * t + P].bitcast(FP8X4),
+                        lhsT_scale=eps_scales[g, G][:, P * t : P * t + P],
+                        rhs=n_codes[k][:, g, cols].bitcast(FP8X4),
+                        rhs_scale=n_scales[k][:, g, cols],
+                        start=(g == 0),
+                        stop=(g == 1),
+                    )
+            k_ps[k, ib, G] = b
+
+        def div_s(k, ib, G):
+            if (ib, G) == (0, 0):
+                jac_bf[k] = wt("jac_bf", [P, 2, ROWS, 4], BF16, 2)
+            b = k_ps.pop((k, ib, G))
+            nc.vector.tensor_tensor(
+                out=jac_bf[k][:, G, P * ib : P * ib + P, :],
+                in0=b[:].rearrange("p t i -> p i t"),
+                in1=rs_row[:, ROWS * k + P * ib : ROWS * k + P * ib + P].unsqueeze(2).to_broadcast([P, P, 4]),
+                op=MULT,
+            )
+
+        def quant_j(k):
+            j_codes[k] = wt("j_codes", [P, 2, ROWS], U32, 2)
+            j_scales[k] = wt("j_scales", [P, 2, ROWS], U8, 2)
+            nc.vector.quantize_mx(
+                out=j_codes[k][:].rearrange("p g i -> p (g i)").bitcast(FP8X4),
+                scales=j_scales[k][:].rearrange("p g i -> p (g i)"),
+                in_=jac_bf[k][:].rearrange("p g i t -> p (g i t)"),
+            )
+
+        o_ps, p_bf = {}, {}
+
+        def stage2(k, h, ib, codes, scales, mat):
+            first = mat == "cu"
+            if first:
+                o_ps[k, h, ib] = bank("s2", [P, 512], F32, 4)
+            cols = slice(P * ib, P * ib + P)
+            for g in range(2):
+                nc.tensor.matmul_mx(
+                    out=o_ps[k, h, ib][:],
+                    lhsT=codes[:, g, cols].bitcast(FP8X4),
+                    lhsT_scale=scales[:, g, cols],
+                    rhs=w_codes[mat, g, h][:].bitcast(FP8X4),
+                    rhs_scale=w_scales[mat, g, h][:],
+                    start=(first and g == 0),
+                    stop=(not first and g == 1),
+                )
+
+        def stage2_l(k, h, ib):
+            stage2(k, h, ib, l_codes[k], l_scales[k], "cu")
+
+        def stage2_j(k, h, ib):
+            stage2(k, h, ib, j_codes[k], j_scales[k], "c")
+
+        def out_rows(k, h, ib, copy):
+            b = o_ps.pop((k, h, ib))
+            p_bf[k, h, ib] = wt("p_bf", [P, 512], BF16, 6)
+            copy(
+                out=p_bf[k, h, ib][:].rearrange("p (u m e) -> p u m e", u=2, e=2),
+                in_=b[:].rearrange("p (m u e) -> p u m e", u=2, e=2),
+            )
+            o_f = wt("o_f", [P, 512], F32, 4)
+            copy(out=o_f[:], in_=b[:])
+            i0 = ROWS * k + P * ib
+            nc.sync.dma_start(out=out_0[i0 : i0 + P, 512 * h : 512 * h + 512], in_=o_f[:])
+
+        pt_bf = {}
+        p_scales = kt("p_scales", [P, 2, D], U8)
+        words_out = out_1.rearrange("g p m t -> g p (m t)").bitcast(I32)
+        scales_out = out_2.bitcast(I32)
+
+        def turn_p(k, h):
+            b = bank("tr", [P, 2, 2, P], F32, TRB)
+            for ib in range(2):
+                words = p_bf.pop((k, h, ib))[:].bitcast(F32)
+                for u in range(2):
+                    nc.tensor.transpose(b[:, u, ib, :], words[:, P * u : P * u + P], ident[:])
+            tr_ps["p", k, h] = b
+
+        def out_p(k, h):
+            b = tr_ps.pop(("p", k, h))
+            pt_bf[k, h] = wt("pt_bf", [P, ROWS, 4], BF16, 3)
+            nc.scalar.copy(
+                out=pt_bf[k, h][:].rearrange("p i t -> p (i t)").bitcast(F32).rearrange("p (i u) -> p i u", u=2),
+                in_=b[:].rearrange("p u b i -> p (b i) u"),
+            )
+
+        def quant_p(k, h):
+            pw = wt("pw", [P, ROWS], U32, 3)
+            nc.vector.quantize_mx(
+                out=pw[:].bitcast(FP8X4),
+                scales=p_scales[:, h, ROWS * k : ROWS * k + ROWS],
+                in_=pt_bf.pop((k, h))[:].rearrange("p i t -> p (i t)"),
+            )
+            nc.sync.dma_start(out=words_out[h, :, ROWS * k : ROWS * k + ROWS], in_=pw[:].bitcast(I32))
+
+        def store_scales(i0, i1):
+            for Q in range(4):
+                nc.sync.dma_start(
+                    out=scales_out[:, 4 * Q : 4 * Q + 4, i0 // 4 : i1 // 4].rearrange("g r i -> r g i"),
+                    in_=p_scales[32 * Q : 32 * Q + 4, :, :].bitcast(I32)[:, :, i0 // 4 : i1 // 4],
+                )
+
+        S_COPY, V_COPY = nc.scalar.copy, nc.vector.tensor_copy
+        spread_e(0)
+        spread_e(1)
+        keep_e(1)
+        mul_e(0, 0, range(4))
+        turn_n(0, 0)
+        turn_n(0, 1)
+        mul_v(0, 0)
+        mul_v(0, 1)
+        inter("cu", 0, 0, "s")
+        spread_rs(0)
+        spread_rs(1)
+        mul_e(1, 1, range(4), True)
+        mul_e(1, 0, range(4))
+        turn_l(0, 0)
+        turn_l(0, 1)
+        out_l(0, 0)
+        out_l(0, 1)
+        inter("cu", 1, 0, "s")
+        quant_n(0)
+        quant_e(0, 0)
+        quant_e(1, 0)
+        stage1(0, 0, 0)
+        stage1(0, 1, 0)
+        mul_e(0, 1, (2, 3), True)
+        mul_e(0, 1, (0, 1))
+        quant_l(0)
+        quant_w("cu", 0, 0)
+        quant_w("cu", 1, 0)
+        inter("c", 0, 0, "s")
+        inter("c", 1, 0, "s")
+        div_s(0, 0, 0)
+        div_s(0, 1, 0)
+        quant_e(1, 1)
+        quant_e(0, 1)
+        stage1(0, 0, 1)
+        stage2_l(0, 0, 0)
+        stage1(0, 1, 1)
+        stage2_l(0, 0, 1)
+        inter("c", 0, 1, "g")
+        inter("c", 1, 1, "g")
+        quant_w("c", 0, 0)
+        div_s(0, 0, 1)
+        div_s(0, 1, 1)
+        quant_w("c", 1, 0)
+        quant_j(0)
+        inter("cu", 0, 1, "s")
+        turn_n(1, 0)
+        turn_n(1, 1)
+        mul_v(1, 0)
+        mul_v(1, 1)
+        inter("cu", 1, 1, "s")
+        quant_n(1)
+
+        for k in range(SB):
+            more = k + 1 < SB
+            more2 = k + 2 < SB
+            last = not more
+            alt = V_COPY if last else S_COPY
+            stage2_j(k, 0, 0)
+            out_rows(k, 0, 0, S_COPY)
+            stage2_j(k, 0, 1)
+            out_rows(k, 0, 1, alt)
+            if k == 0:
+                turn_l(1, 0)
+                turn_l(1, 1)
+                out_l(1, 0)
+                out_l(1, 1)
+                stage1(1, 0, 0)
+                quant_w("cu", 0, 1)
+                quant_w("c", 0, 1)
+                div_s(1, 0, 0)
+                stage1(1, 1, 0)
+                div_s(1, 1, 0)
+                quant_w("cu", 1, 1)
+                quant_w("c", 1, 1)
+                quant_l(1)
+                stage2_l(0, 1, 0)
+                stage2_j(0, 1, 0)
+                out_rows(0, 1, 0, S_COPY)
+                stage2_l(0, 1, 1)
+                stage2_j(0, 1, 1)
+                out_rows(0, 1, 1, S_COPY)
+            else:
+                if more:
+                    stage1(k + 1, 0, 0)
+                    div_s(k + 1, 0, 0)
+                    quant_p(k - 1, 1)
+                stage2_j(k, 1, 0)
+                if last:
+                    quant_p(k - 1, 1)
+                    store_scales(0, ROWS * k)
+                    turn_p(k, 0)
+                    out_p(k, 0)
+                out_rows(k, 1, 0, S_COPY)
+                if more:
+                    stage1(k + 1, 1, 0)
+                    div_s(k + 1, 1, 0)
+                    quant_l(k + 1)
+                stage2_j(k, 1, 1)
+                out_rows(k, 1, 1, alt)
+            if more2:
+                turn_n(k + 2, 0)
+                turn_n(k + 2, 1)
+                mul_v(k + 2, 0)
+                mul_v(k + 2, 1)
+            if more:
+                stage1(k + 1, 0, 1)
+                div_s(k + 1, 0, 1)
+                stage1(k + 1, 1, 1)
+                div_s(k + 1, 1, 1)
+                quant_j(k + 1)
+            if more:
+                turn_p(k, 0)
+                out_p(k, 0)
+            if more2:
+                turn_l(k + 2, 0)
+                out_l(k + 2, 0)
+            if more:
+                stage2_l(k + 1, 0, 0)
+                stage2_l(k + 1, 0, 1)
+            if more2:
+                quant_n(k + 2)
+            quant_p(k, 0)
+            turn_p(k, 1)
+            out_p(k, 1)
+            if more2:
+                turn_l(k + 2, 1)
+                out_l(k + 2, 1)
+            if more:
+                stage2_l(k + 1, 1, 0)
+                stage2_l(k + 1, 1, 1)
+        quant_p(SB - 1, 1)
+        store_scales(ROWS * (SB - 1), D)

@@ -58,13 +58,9 @@ def tile_relativefluctuationcovariancedrift_kernel(tc, n, v, a, s, c, l, cu, out
         for k in range(SB):
             n_raw.append(kt("n_raw%d" % k, [P, 2, D], BF16))
             l_raw.append(kt("l_raw%d" % k, [P, 2, D], BF16))
-        a_raw = {}
-        cu_raw = {}
-        for g in range(2):
-            for h in range(2):
-                a_raw[g, h] = kt("a_raw%d%d" % (g, h), [P, 4, 512], BF16)
-                cu_raw[g, h] = kt("cu_raw%d%d" % (g, h), [P, 4, 512], BF16)
-        c_raw = {(g, h): kt("c_raw%d%d" % (g, h), [P, 4, 512], BF16) for g in range(2) for h in range(2)}
+        a_raw = [kt("a_raw%d" % g, [P, 4, D], BF16) for g in range(2)]
+        cu_raw = [kt("cu_raw%d" % g, [P, 4, D], BF16) for g in range(2)]
+        c_raw = [kt("c_raw%d" % g, [P, 4, D], BF16) for g in range(2)]
 
         def load_n(k):
             nc.sync.dma_start(out=n_raw[k][:], in_=n[ROWS * k : ROWS * k + ROWS, :].rearrange("(b p) r -> p b r", p=P))
@@ -72,37 +68,20 @@ def tile_relativefluctuationcovariancedrift_kernel(tc, n, v, a, s, c, l, cu, out
         def load_l(k):
             nc.sync.dma_start(out=l_raw[k][:], in_=l[ROWS * k : ROWS * k + ROWS, :].rearrange("(b p) r -> p b r", p=P))
 
-        def load_part(raw, src, g, h):
-            nc.sync.dma_start(
-                out=raw[g, h][:],
-                in_=src[512 * g : 512 * g + 512, 512 * h : 512 * h + 512].rearrange("(p j) w -> p j w", j=4),
-            )
+        def load_a(g):
+            load_w(a_raw, a, g)
 
-        def load_c(g, h):
-            rows = c[512 * g : 512 * g + 512, 512 * h : 512 * h + 512].rearrange("(b t q) z -> t b q z", t=4, q=8)
+        def load_cu(g):
+            load_w(cu_raw, cu, g)
+
+        def load_w(raw, src, g):
+            nc.sync.dma_start(out=raw[g][:], in_=src[512 * g : 512 * g + 512, :].rearrange("(p j) w -> p j w", j=4))
+
+        def load_c(g):
+            rows = c[512 * g : 512 * g + 512, :].rearrange("(b t q) z -> t b q z", t=4, q=8)
             for t in range(4):
-                nc.sync.dma_start(out=c_raw[g, h][:, t, :], in_=rows[t])
+                nc.sync.dma_start(out=c_raw[g][:, t, :], in_=rows[t])
 
-        load_part(a_raw, a, 0, 0)
-        load_part(cu_raw, cu, 0, 0)
-        load_n(0)
-        load_part(a_raw, a, 1, 0)
-        load_part(a_raw, a, 1, 1)
-        load_l(0)
-        load_part(cu_raw, cu, 1, 0)
-        load_part(a_raw, a, 0, 1)
-        load_c(0, 0)
-        load_c(1, 0)
-        load_n(1)
-        load_c(0, 1)
-        load_part(cu_raw, cu, 0, 1)
-        load_c(1, 1)
-        load_part(cu_raw, cu, 1, 1)
-        load_l(1)
-        load_n(2)
-        load_l(2)
-        load_n(3)
-        load_l(3)
 
         s_ps = bank("tr", [P, P], BF16, TRB)
         nc.tensor.transpose(s_ps[:], srow[:], identb[:])
@@ -152,7 +131,7 @@ def tile_relativefluctuationcovariancedrift_kernel(tc, n, v, a, s, c, l, cu, out
         l_bf, l_codes, l_scales = {}, {}, {}
 
         def mul_v(k, g):
-            if g == 0:
+            if k not in nv_bf:
                 nv_bf[k] = wt("nv_bf", [P, 2, ROWS, 4], BF16, 2)
             b = tr_ps.pop(("n", k, g))
             nc.vector.tensor_tensor(
@@ -171,11 +150,11 @@ def tile_relativefluctuationcovariancedrift_kernel(tc, n, v, a, s, c, l, cu, out
                 in_=nv_bf[k][:].rearrange("p g i t -> p (g i t)"),
             )
 
-        def out_l(k, g):
-            if g == 0:
+        def out_l(k, g, copy):
+            if k not in l_bf:
                 l_bf[k] = wt("l_bf", [P, 2, ROWS, 4], BF16, 3)
             b = tr_ps.pop(("l", k, g))
-            nc.scalar.copy(
+            copy(
                 out=l_bf[k][:, g].rearrange("p i t -> p (i t)").bitcast(F32).rearrange("p (i u) -> p i u", u=2),
                 in_=b[:].rearrange("p u b i -> p (b i) u"),
             )
@@ -203,7 +182,7 @@ def tile_relativefluctuationcovariancedrift_kernel(tc, n, v, a, s, c, l, cu, out
                 e_t = e_row[:, t] if on_gpsimd else e_ps[G][:, t]
                 (nc.gpsimd if on_gpsimd else nc.vector).tensor_tensor(
                     out=eps_bf[g, G][:, t].rearrange("p (b q) j -> p b q j", q=8),
-                    in0=a_raw[g, G][:].rearrange("p j (b t q) -> p t b q j", t=4, q=8)[:, t],
+                    in0=a_raw[g][:, :, 512 * G : 512 * G + 512].rearrange("p j (b t q) -> p t b q j", t=4, q=8)[:, t],
                     in1=e_t.rearrange("p (b q) -> p b q", q=8).unsqueeze(3).to_broadcast([P, 16, 8, 4]),
                     op=MULT,
                 )
@@ -222,7 +201,7 @@ def tile_relativefluctuationcovariancedrift_kernel(tc, n, v, a, s, c, l, cu, out
         def inter(mat, g, h, engine):
             dst = wt("w_bf", [P, 512, 4], BF16, 6)
             w_bf[mat, g, h] = dst
-            src = cu_raw[g, h][:] if mat == "cu" else c_raw[g, h][:]
+            src = (cu_raw if mat == "cu" else c_raw)[g][:, :, 512 * h : 512 * h + 512]
             if engine == "s":
                 nc.scalar.copy(
                     out=dst[:].rearrange("p (x i) j -> p x j i", i=4),
@@ -273,7 +252,7 @@ def tile_relativefluctuationcovariancedrift_kernel(tc, n, v, a, s, c, l, cu, out
             k_ps[k, ib, G] = b
 
         def div_s(k, ib, G):
-            if (ib, G) == (0, 0):
+            if k not in jac_bf:
                 jac_bf[k] = wt("jac_bf", [P, 2, ROWS, 4], BF16, 2)
             b = k_ps.pop((k, ib, G))
             nc.vector.tensor_tensor(
@@ -316,15 +295,21 @@ def tile_relativefluctuationcovariancedrift_kernel(tc, n, v, a, s, c, l, cu, out
         def stage2_j(k, h, ib):
             stage2(k, h, ib, j_codes[k], j_scales[k], "c")
 
-        def out_rows(k, h, ib, copy):
+        def out_rows(k, h, ib, copy, round_v=False):
             b = o_ps.pop((k, h, ib))
             p_bf[k, h, ib] = wt("p_bf", [P, 512], BF16, 6)
-            copy(
-                out=p_bf[k, h, ib][:].rearrange("p (u m e) -> p u m e", u=2, e=2),
-                in_=b[:].rearrange("p (m u e) -> p u m e", u=2, e=2),
-            )
             o_f = wt("o_f", [P, 512], F32, 4)
-            copy(out=o_f[:], in_=b[:])
+
+            def turned(t):
+                return t[:].rearrange("p (m u e) -> p u m e", u=2, e=2)
+
+            to = p_bf[k, h, ib][:].rearrange("p (u m e) -> p u m e", u=2, e=2)
+            if round_v:
+                copy(out=o_f[:], in_=b[:])
+                nc.vector.tensor_copy(out=to, in_=turned(o_f))
+            else:
+                copy(out=to, in_=turned(b))
+                copy(out=o_f[:], in_=b[:])
             i0 = ROWS * k + P * ib
             nc.sync.dma_start(out=out_0[i0 : i0 + P, 512 * h : 512 * h + 512], in_=o_f[:])
 
@@ -341,10 +326,10 @@ def tile_relativefluctuationcovariancedrift_kernel(tc, n, v, a, s, c, l, cu, out
                     nc.tensor.transpose(b[:, u, ib, :], words[:, P * u : P * u + P], ident[:])
             tr_ps["p", k, h] = b
 
-        def out_p(k, h):
+        def out_p(k, h, copy):
             b = tr_ps.pop(("p", k, h))
             pt_bf[k, h] = wt("pt_bf", [P, ROWS, 4], BF16, 3)
-            nc.scalar.copy(
+            copy(
                 out=pt_bf[k, h][:].rearrange("p i t -> p (i t)").bitcast(F32).rearrange("p (i u) -> p i u", u=2),
                 in_=b[:].rearrange("p u b i -> p (b i) u"),
             )
@@ -366,136 +351,196 @@ def tile_relativefluctuationcovariancedrift_kernel(tc, n, v, a, s, c, l, cu, out
                 )
 
         S_COPY, V_COPY = nc.scalar.copy, nc.vector.tensor_copy
+        T4 = range(4)
+        load_a(0)
+        load_l(0)
         spread_e(0)
         spread_e(1)
-        keep_e(1)
-        mul_e(0, 0, range(4))
+        load_n(0)
+        load_a(1)
+        load_cu(1)
+        mul_e(0, 0, T4)
+        turn_l(0, 0)
+        spread_rs(1)
+        load_cu(0)
         turn_n(0, 0)
+        out_l(0, 0, S_COPY)
+        mul_e(0, 1, T4)
+        load_n(1)
+        quant_e(0, 0)
+        spread_rs(0)
         turn_n(0, 1)
         mul_v(0, 0)
-        mul_v(0, 1)
-        inter("cu", 0, 0, "s")
-        spread_rs(0)
-        spread_rs(1)
-        mul_e(1, 1, range(4), True)
-        mul_e(1, 0, range(4))
-        turn_l(0, 0)
-        turn_l(0, 1)
-        out_l(0, 0)
-        out_l(0, 1)
-        inter("cu", 1, 0, "s")
-        quant_n(0)
-        quant_e(0, 0)
-        quant_e(1, 0)
-        stage1(0, 0, 0)
-        stage1(0, 1, 0)
-        mul_e(0, 1, (2, 3), True)
-        mul_e(0, 1, (0, 1))
-        quant_l(0)
-        quant_w("cu", 0, 0)
-        quant_w("cu", 1, 0)
-        inter("c", 0, 0, "s")
-        inter("c", 1, 0, "s")
-        div_s(0, 0, 0)
-        div_s(0, 1, 0)
-        quant_e(1, 1)
-        quant_e(0, 1)
-        stage1(0, 0, 1)
-        stage2_l(0, 0, 0)
-        stage1(0, 1, 1)
-        stage2_l(0, 0, 1)
-        inter("c", 0, 1, "g")
-        inter("c", 1, 1, "g")
-        quant_w("c", 0, 0)
-        div_s(0, 0, 1)
-        div_s(0, 1, 1)
-        quant_w("c", 1, 0)
-        quant_j(0)
-        inter("cu", 0, 1, "s")
-        turn_n(1, 0)
+        load_l(1)
         turn_n(1, 1)
-        mul_v(1, 0)
+        mul_e(1, 0, T4)
+        inter("cu", 1, 0, "s")
+        mul_v(0, 1)
+        mul_e(1, 1, T4)
+        load_n(2)
+        inter("cu", 0, 0, "s")
+        turn_l(0, 1)
+        out_l(0, 1, S_COPY)
         mul_v(1, 1)
-        inter("cu", 1, 1, "s")
+        turn_l(1, 0)
+        quant_e(0, 1)
+        out_l(1, 0, S_COPY)
+        turn_n(1, 0)
+        load_c(0)
+        quant_e(1, 1)
+        turn_n(2, 1)
+        quant_n(0)
+        load_n(3)
+        mul_v(1, 0)
+        quant_e(1, 0)
+        load_c(1)
+        mul_v(2, 1)
+        stage1(0, 0, 1)
+        inter("cu", 0, 1, "s")
+        turn_l(1, 1)
+        div_s(0, 0, 1)
+        stage1(0, 0, 0)
+        turn_n(2, 0)
         quant_n(1)
-
-        for k in range(SB):
-            more = k + 1 < SB
-            more2 = k + 2 < SB
-            last = not more
-            alt = V_COPY if last else S_COPY
-            stage2_j(k, 0, 0)
-            out_rows(k, 0, 0, S_COPY)
-            stage2_j(k, 0, 1)
-            out_rows(k, 0, 1, alt)
-            if k == 0:
-                turn_l(1, 0)
-                turn_l(1, 1)
-                out_l(1, 0)
-                out_l(1, 1)
-                stage1(1, 0, 0)
-                quant_w("cu", 0, 1)
-                quant_w("c", 0, 1)
-                div_s(1, 0, 0)
-                stage1(1, 1, 0)
-                div_s(1, 1, 0)
-                quant_w("cu", 1, 1)
-                quant_w("c", 1, 1)
-                quant_l(1)
-                stage2_l(0, 1, 0)
-                stage2_j(0, 1, 0)
-                out_rows(0, 1, 0, S_COPY)
-                stage2_l(0, 1, 1)
-                stage2_j(0, 1, 1)
-                out_rows(0, 1, 1, S_COPY)
-            else:
-                if more:
-                    stage1(k + 1, 0, 0)
-                    div_s(k + 1, 0, 0)
-                    quant_p(k - 1, 1)
-                stage2_j(k, 1, 0)
-                if last:
-                    quant_p(k - 1, 1)
-                    store_scales(0, ROWS * k)
-                    turn_p(k, 0)
-                    out_p(k, 0)
-                out_rows(k, 1, 0, S_COPY)
-                if more:
-                    stage1(k + 1, 1, 0)
-                    div_s(k + 1, 1, 0)
-                    quant_l(k + 1)
-                stage2_j(k, 1, 1)
-                out_rows(k, 1, 1, alt)
-            if more2:
-                turn_n(k + 2, 0)
-                turn_n(k + 2, 1)
-                mul_v(k + 2, 0)
-                mul_v(k + 2, 1)
-            if more:
-                stage1(k + 1, 0, 1)
-                div_s(k + 1, 0, 1)
-                stage1(k + 1, 1, 1)
-                div_s(k + 1, 1, 1)
-                quant_j(k + 1)
-            if more:
-                turn_p(k, 0)
-                out_p(k, 0)
-            if more2:
-                turn_l(k + 2, 0)
-                out_l(k + 2, 0)
-            if more:
-                stage2_l(k + 1, 0, 0)
-                stage2_l(k + 1, 0, 1)
-            if more2:
-                quant_n(k + 2)
-            quant_p(k, 0)
-            turn_p(k, 1)
-            out_p(k, 1)
-            if more2:
-                turn_l(k + 2, 1)
-                out_l(k + 2, 1)
-            if more:
-                stage2_l(k + 1, 1, 0)
-                stage2_l(k + 1, 1, 1)
-        quant_p(SB - 1, 1)
-        store_scales(ROWS * (SB - 1), D)
+        div_s(0, 0, 0)
+        stage1(0, 1, 1)
+        mul_v(2, 0)
+        load_l(2)
+        stage1(0, 1, 0)
+        out_l(1, 1, S_COPY)
+        load_l(3)
+        turn_n(3, 0)
+        inter("c", 0, 0, "s")
+        div_s(0, 1, 1)
+        div_s(0, 1, 0)
+        quant_w("cu", 0, 0)
+        quant_l(0)
+        stage1(1, 1, 0)
+        quant_w("cu", 1, 0)
+        div_s(1, 1, 0)
+        turn_n(3, 1)
+        stage1(1, 0, 0)
+        mul_v(3, 0)
+        stage2_l(0, 0, 0)
+        mul_v(3, 1)
+        stage2_l(0, 0, 1)
+        inter("c", 1, 1, "s")
+        div_s(1, 0, 0)
+        stage1(1, 0, 1)
+        div_s(1, 0, 1)
+        turn_l(2, 1)
+        turn_l(3, 1)
+        inter("c", 1, 0, "s")
+        stage1(1, 1, 1)
+        quant_l(1)
+        out_l(2, 1, S_COPY)
+        out_l(3, 1, S_COPY)
+        turn_l(3, 0)
+        quant_n(2)
+        turn_l(2, 0)
+        quant_j(0)
+        div_s(1, 1, 1)
+        stage1(2, 0, 0)
+        quant_w("c", 1, 0)
+        stage2_l(1, 0, 0)
+        quant_w("c", 0, 0)
+        inter("cu", 1, 1, "s")
+        stage2_l(1, 0, 1)
+        div_s(2, 0, 0)
+        stage1(2, 0, 1)
+        stage2_j(0, 0, 1)
+        quant_j(1)
+        inter("c", 0, 1, "s")
+        stage2_j(0, 0, 0)
+        stage1(2, 1, 0)
+        stage2_j(1, 0, 1)
+        stage2_j(1, 0, 0)
+        quant_w("cu", 1, 1)
+        div_s(2, 0, 1)
+        stage1(2, 1, 1)
+        quant_w("cu", 0, 1)
+        quant_w("c", 0, 1)
+        out_rows(0, 0, 0, S_COPY, True)
+        quant_w("c", 1, 1)
+        div_s(2, 1, 0)
+        out_rows(0, 0, 1, S_COPY)
+        stage2_l(1, 1, 0)
+        stage2_j(1, 1, 0)
+        stage2_l(0, 1, 0)
+        out_rows(1, 0, 0, S_COPY, True)
+        out_l(2, 0, V_COPY)
+        div_s(2, 1, 1)
+        stage2_j(0, 1, 0)
+        stage2_l(0, 1, 1)
+        out_l(3, 0, S_COPY)
+        out_rows(1, 0, 1, S_COPY, True)
+        stage2_l(1, 1, 1)
+        turn_p(1, 0)
+        turn_p(0, 0)
+        stage2_j(0, 1, 1)
+        out_p(1, 0, S_COPY)
+        quant_n(3)
+        stage1(3, 1, 0)
+        out_rows(1, 1, 0, S_COPY)
+        div_s(3, 1, 0)
+        quant_l(2)
+        stage1(3, 0, 0)
+        out_rows(0, 1, 1, S_COPY, True)
+        stage2_j(1, 1, 1)
+        stage1(3, 0, 1)
+        out_rows(0, 1, 0, S_COPY, True)
+        out_p(0, 0, S_COPY)
+        div_s(3, 0, 0)
+        quant_p(1, 0)
+        div_s(3, 0, 1)
+        stage2_l(2, 0, 0)
+        out_rows(1, 1, 1, S_COPY, True)
+        quant_j(2)
+        stage2_l(2, 1, 1)
+        stage2_l(2, 0, 1)
+        stage2_l(2, 1, 0)
+        turn_p(1, 1)
+        turn_p(0, 1)
+        stage2_j(2, 0, 0)
+        stage2_j(2, 1, 1)
+        out_p(0, 1, S_COPY)
+        quant_p(0, 0)
+        quant_l(3)
+        out_rows(2, 0, 0, V_COPY)
+        stage2_j(2, 1, 0)
+        stage2_j(2, 0, 1)
+        stage1(3, 1, 1)
+        out_p(1, 1, V_COPY)
+        stage2_l(3, 0, 0)
+        out_rows(2, 1, 1, S_COPY)
+        quant_p(0, 1)
+        div_s(3, 1, 1)
+        out_rows(2, 0, 1, S_COPY, True)
+        out_rows(2, 1, 0, S_COPY)
+        quant_j(3)
+        stage2_l(3, 1, 1)
+        quant_p(1, 1)
+        turn_p(2, 1)
+        turn_p(2, 0)
+        out_p(2, 1, S_COPY)
+        stage2_j(3, 1, 1)
+        stage2_l(3, 1, 0)
+        quant_p(2, 1)
+        stage2_j(3, 0, 0)
+        out_p(2, 0, S_COPY)
+        quant_p(2, 0)
+        stage2_l(3, 0, 1)
+        out_rows(3, 1, 1, S_COPY, True)
+        stage2_j(3, 0, 1)
+        out_rows(3, 0, 0, S_COPY, True)
+        store_scales(0, ROWS * 3)
+        out_rows(3, 0, 1, V_COPY)
+        stage2_j(3, 1, 0)
+        turn_p(3, 0)
+        out_rows(3, 1, 0, S_COPY, True)
+        turn_p(3, 1)
+        out_p(3, 0, S_COPY)
+        out_p(3, 1, S_COPY)
+        quant_p(3, 0)
+        quant_p(3, 1)
+        store_scales(ROWS * 3, D)

@@ -19,6 +19,8 @@ P = 128
 SB = 4
 ROWS = 256
 TRB = 2
+S1B = 2
+S2B = 4
 
 
 def tile_relativefluctuationcovariancedrift_kernel(tc, n, v, a, s, c, l, cu, out_0, out_1, out_2):
@@ -51,21 +53,19 @@ def tile_relativefluctuationcovariancedrift_kernel(tc, n, v, a, s, c, l, cu, out
                 in_=s[512 * g : 512 * g + 512].rearrange("(b t q) -> t b q", t=4, q=8),
             )
         nc.sync.dma_start(out=srow[8:16, :], in_=s.rearrange("(x p) -> x p", p=P))
-        v4 = kt("v4", [P, 2, 4], BF16)
-        nc.sync.dma_start(out=v4[:], in_=v.rearrange("(g p j) -> p g j", p=P, j=4))
+        nc.sync.dma_start(out=srow[16:24, :], in_=v.rearrange("(x p) -> x p", p=P))
 
-        n_raw, l_raw = [], []
-        for k in range(SB):
-            n_raw.append(kt("n_raw%d" % k, [P, 2, D], BF16))
-            l_raw.append(kt("l_raw%d" % k, [P, 2, D], BF16))
+        n_raw, l_raw = {}, {}
         a_raw = [kt("a_raw%d" % g, [P, 4, D], BF16) for g in range(2)]
         cu_raw = [kt("cu_raw%d" % g, [P, 4, D], BF16) for g in range(2)]
         c_raw = [kt("c_raw%d" % g, [P, 4, D], BF16) for g in range(2)]
 
         def load_n(k):
+            n_raw[k] = wt("n_raw", [P, 2, D], BF16, 3)
             nc.sync.dma_start(out=n_raw[k][:], in_=n[ROWS * k : ROWS * k + ROWS, :].rearrange("(b p) r -> p b r", p=P))
 
         def load_l(k):
+            l_raw[k] = wt("l_raw", [P, 2, D], BF16, 3)
             nc.sync.dma_start(out=l_raw[k][:], in_=l[ROWS * k : ROWS * k + ROWS, :].rearrange("(b p) r -> p b r", p=P))
 
         def load_a(g):
@@ -96,10 +96,20 @@ def tile_relativefluctuationcovariancedrift_kernel(tc, n, v, a, s, c, l, cu, out
         rs8 = kt("rs8", [P, 8], F32)
         nc.vector.reciprocal(out=rs8[:], in_=s_cols[:, 8:16])
 
+        v_cols = kt("v_cols", [P, 8], BF16)
+        nc.vector.tensor_copy(out=v_cols[:], in_=s_ps[:, 16:24])
+        v_row = kt("v_row", [P, D], BF16)
+
+        def spread_v():
+            b = bank("tr", [P, 8, P], BF16, TRB)
+            for x in range(8):
+                nc.tensor.transpose(b[:, x, :], v_cols[:, x : x + 1].to_broadcast([P, P]), identb[:])
+            nc.scalar.copy(out=v_row[:], in_=b[:].rearrange("p x i -> p (x i)"))
+
         e_ps = {}
 
         def spread_e(G):
-            e_ps[G] = bank("s2", [P, 4, P], F32, 4)
+            e_ps[G] = bank("s2", [P, 4, P], F32, S2B)
             for t in range(4):
                 j = 4 * G + t
                 nc.tensor.transpose(e_ps[G][:, t, :], e4[:, j : j + 1].to_broadcast([P, P]), ident[:])
@@ -107,38 +117,52 @@ def tile_relativefluctuationcovariancedrift_kernel(tc, n, v, a, s, c, l, cu, out
         rs_row = kt("rs_row", [P, D], F32)
 
         def spread_rs(y):
-            b = bank("s1", [P, 4, P], F32, 2)
+            b = bank("s1", [P, 4, P], F32, S1B)
             for x in range(4):
                 nc.tensor.transpose(b[:, x, :], rs8[:, 4 * y + x : 4 * y + x + 1].to_broadcast([P, P]), ident[:])
             nc.scalar.copy(out=rs_row[:, 512 * y : 512 * y + 512], in_=b[:].rearrange("p x i -> p (x i)"))
 
         tr_ps = {}
 
-        def turn(key, words, g):
+        def turn_l(k, g):
             b = bank("tr", [P, 2, 2, P], F32, TRB)
+            words = l_raw[k][:].bitcast(F32)
             for u in range(2):
                 for ib in range(2):
                     nc.tensor.transpose(b[:, u, ib, :], words[:, ib, 256 * g + u : 256 * g + 256 : 2], ident[:])
-            tr_ps[key] = b
+            tr_ps["l", k, g] = b
 
-        def turn_n(k, g):
-            turn(("n", k, g), n_raw[k][:].bitcast(F32), g)
-
-        def turn_l(k, g):
-            turn(("l", k, g), l_raw[k][:].bitcast(F32), g)
-
-        nv_bf, n_codes, n_scales = {}, {}, {}
+        nv, n_bf, n_codes, n_scales = {}, {}, {}, {}
         l_bf, l_codes, l_scales = {}, {}, {}
 
-        def mul_v(k, g):
-            if k not in nv_bf:
-                nv_bf[k] = wt("nv_bf", [P, 2, ROWS, 4], BF16, 2)
+        def mul_n(k, ib, eng):
+            if k not in nv:
+                nv[k] = wt("nv", [P, 2, D], BF16, 2)
+            for g in range(2):
+                cols = slice(512 * g, 512 * g + 512)
+                eng.tensor_tensor(
+                    out=nv[k][:, ib, cols].rearrange("p (u m e) -> p u m e", u=2, e=2),
+                    in0=n_raw[k][:, ib, cols].rearrange("p (m u e) -> p u m e", u=2, e=2),
+                    in1=v_row[:, cols].rearrange("p (m u e) -> p u m e", u=2, e=2),
+                    op=MULT,
+                )
+
+        def turn_n(k, g):
+            b = bank("tr", [P, 2, 2, P], F32, TRB)
+            words = nv[k][:].bitcast(F32)
+            for u in range(2):
+                for ib in range(2):
+                    w0 = 256 * g + 128 * u
+                    nc.tensor.transpose(b[:, u, ib, :], words[:, ib, w0 : w0 + 128], ident[:])
+            tr_ps["n", k, g] = b
+
+        def out_n(k, g, copy):
+            if k not in n_bf:
+                n_bf[k] = wt("n_bf", [P, 2, ROWS, 4], BF16, 2)
             b = tr_ps.pop(("n", k, g))
-            nc.vector.tensor_tensor(
-                out=nv_bf[k][:, g].rearrange("p i (u e) -> p i u e", u=2),
-                in0=b[:].rearrange("p u b i -> p (u b i)").bitcast(BF16).rearrange("p (u i e) -> p i u e", u=2, e=2),
-                in1=v4[:, g].rearrange("p (u e) -> p u e", u=2).unsqueeze(1).to_broadcast([P, ROWS, 2, 2]),
-                op=MULT,
+            copy(
+                out=n_bf[k][:, g].rearrange("p i t -> p (i t)").bitcast(F32).rearrange("p (i u) -> p i u", u=2),
+                in_=b[:].rearrange("p u b i -> p (b i) u"),
             )
 
         def quant_n(k):
@@ -147,7 +171,7 @@ def tile_relativefluctuationcovariancedrift_kernel(tc, n, v, a, s, c, l, cu, out
             nc.vector.quantize_mx(
                 out=n_codes[k][:].rearrange("p g i -> p (g i)").bitcast(FP8X4),
                 scales=n_scales[k][:].rearrange("p g i -> p (g i)"),
-                in_=nv_bf[k][:].rearrange("p g i t -> p (g i t)"),
+                in_=n_bf[k][:].rearrange("p g i t -> p (g i t)"),
             )
 
         def out_l(k, g, copy):
@@ -170,22 +194,24 @@ def tile_relativefluctuationcovariancedrift_kernel(tc, n, v, a, s, c, l, cu, out
 
         eps_bf, eps_codes, eps_scales = {}, {}, {}
 
-        e_row = kt("e_row", [P, 4, P], F32)
+        e_row = {}
 
         def keep_e(G):
-            nc.scalar.copy(out=e_row[:].rearrange("p t m -> p (t m)"), in_=e_ps[G][:].rearrange("p t m -> p (t m)"))
+            e_row[G] = kt("e_row%d" % G, [P, 4, P], F32)
+            nc.scalar.copy(out=e_row[G][:].rearrange("p t m -> p (t m)"), in_=e_ps[G][:].rearrange("p t m -> p (t m)"))
 
-        def mul_e(g, G, ts, on_gpsimd=False):
+        def mul_e(g, G, t, on_gpsimd=False):
             if (g, G) not in eps_bf:
                 eps_bf[g, G] = wt("eps_bf", [P, 4, P, 4], BF16, 3)
-            for t in ts:
-                e_t = e_row[:, t] if on_gpsimd else e_ps[G][:, t]
-                (nc.gpsimd if on_gpsimd else nc.vector).tensor_tensor(
-                    out=eps_bf[g, G][:, t].rearrange("p (b q) j -> p b q j", q=8),
-                    in0=a_raw[g][:, :, 512 * G : 512 * G + 512].rearrange("p j (b t q) -> p t b q j", t=4, q=8)[:, t],
-                    in1=e_t.rearrange("p (b q) -> p b q", q=8).unsqueeze(3).to_broadcast([P, 16, 8, 4]),
-                    op=MULT,
-                )
+            e_t = e_row[G][:, t] if on_gpsimd else e_ps[G][:, t]
+            out = eps_bf[g, G][:, t].rearrange("p (b q) j -> p b q j", q=8)
+            in0 = a_raw[g][:, :, 512 * G : 512 * G + 512].rearrange("p j (b t q) -> p t b q j", t=4, q=8)[:, t]
+            in1 = e_t.rearrange("p (b q) -> p b q", q=8).unsqueeze(3).to_broadcast([P, 16, 8, 4])
+            if on_gpsimd:
+                for b in (slice(0, 8), slice(8, 16)):
+                    nc.gpsimd.tensor_tensor(out=out[:, b], in0=in0[:, b], in1=in1[:, b], op=MULT)
+            else:
+                nc.vector.tensor_tensor(out=out, in0=in0, in1=in1, op=MULT)
 
         def quant_e(g, G):
             eps_codes[g, G] = kt("eps_codes%d%d" % (g, G), [P, 512], U32)
@@ -236,7 +262,7 @@ def tile_relativefluctuationcovariancedrift_kernel(tc, n, v, a, s, c, l, cu, out
         k_ps, jac_bf, j_codes, j_scales = {}, {}, {}, {}
 
         def stage1(k, ib, G):
-            b = bank("s1", [P, 4, P], F32, 2)
+            b = bank("s1", [P, 4, P], F32, S1B)
             cols = slice(P * ib, P * ib + P)
             for t in range(4):
                 for g in range(2):
@@ -276,7 +302,7 @@ def tile_relativefluctuationcovariancedrift_kernel(tc, n, v, a, s, c, l, cu, out
         def stage2(k, h, ib, codes, scales, mat):
             first = mat == "cu"
             if first:
-                o_ps[k, h, ib] = bank("s2", [P, 512], F32, 4)
+                o_ps[k, h, ib] = bank("s2", [P, 512], F32, S2B)
             cols = slice(P * ib, P * ib + P)
             for g in range(2):
                 nc.tensor.matmul_mx(
@@ -352,195 +378,218 @@ def tile_relativefluctuationcovariancedrift_kernel(tc, n, v, a, s, c, l, cu, out
 
         S_COPY, V_COPY = nc.scalar.copy, nc.vector.tensor_copy
         T4 = range(4)
+        load_a(1)
+        spread_e(1)
+        spread_e(0)
+        keep_e(1)
         load_a(0)
         load_l(0)
-        spread_e(0)
-        spread_e(1)
         load_n(0)
-        load_a(1)
-        load_cu(1)
-        mul_e(0, 0, T4)
-        turn_l(0, 0)
-        spread_rs(1)
-        load_cu(0)
-        turn_n(0, 0)
-        out_l(0, 0, S_COPY)
-        mul_e(0, 1, T4)
+        mul_e(1, 1, 0)
+        mul_e(1, 1, 2)
         load_n(1)
-        quant_e(0, 0)
-        spread_rs(0)
-        turn_n(0, 1)
-        mul_v(0, 0)
-        load_l(1)
-        turn_n(1, 1)
-        mul_e(1, 0, T4)
-        inter("cu", 1, 0, "s")
-        mul_v(0, 1)
-        mul_e(1, 1, T4)
-        load_n(2)
-        inter("cu", 0, 0, "s")
-        turn_l(0, 1)
-        out_l(0, 1, S_COPY)
-        mul_v(1, 1)
-        turn_l(1, 0)
-        quant_e(0, 1)
-        out_l(1, 0, S_COPY)
-        turn_n(1, 0)
-        load_c(0)
+        mul_e(1, 1, 1, True)
+        mul_e(1, 1, 3)
+        load_cu(1)
+        mul_e(0, 1, 2)
+        keep_e(0)
         quant_e(1, 1)
-        turn_n(2, 1)
-        quant_n(0)
+        spread_v()
+        mul_e(0, 1, 1)
+        mul_e(0, 1, 3, True)
+        mul_e(1, 0, 3)
+        load_l(1)
+        mul_e(1, 0, 0)
+        mul_n(0, 1, nc.vector)
+        mul_n(0, 0, nc.vector)
+        mul_e(1, 0, 1)
+        mul_e(0, 1, 0, True)
+        load_n(2)
+        spread_rs(1)
         load_n(3)
-        mul_v(1, 0)
-        quant_e(1, 0)
-        load_c(1)
-        mul_v(2, 1)
-        stage1(0, 0, 1)
-        inter("cu", 0, 1, "s")
-        turn_l(1, 1)
-        div_s(0, 0, 1)
-        stage1(0, 0, 0)
-        turn_n(2, 0)
-        quant_n(1)
-        div_s(0, 0, 0)
-        stage1(0, 1, 1)
-        mul_v(2, 0)
-        load_l(2)
-        stage1(0, 1, 0)
-        out_l(1, 1, S_COPY)
+        spread_rs(0)
+        mul_n(1, 1, nc.vector)
+        turn_l(0, 1)
+        turn_l(0, 0)
+        out_l(0, 1, S_COPY)
+        mul_e(0, 0, 2, True)
+        turn_n(0, 1)
+        mul_n(1, 0, nc.vector)
+        mul_e(0, 0, 3)
+        quant_e(0, 1)
+        out_l(0, 0, S_COPY)
+        out_n(0, 1, S_COPY)
+        turn_n(0, 0)
+        mul_e(1, 0, 2, True)
+        turn_n(1, 1)
+        out_n(0, 0, S_COPY)
         load_l(3)
-        turn_n(3, 0)
-        inter("c", 0, 0, "s")
-        div_s(0, 1, 1)
-        div_s(0, 1, 0)
-        quant_w("cu", 0, 0)
+        out_n(1, 1, S_COPY)
+        mul_e(0, 0, 1)
+        turn_n(1, 0)
+        inter("cu", 1, 0, "s")
+        mul_e(0, 0, 0, True)
+        quant_n(0)
+        turn_l(1, 0)
+        quant_e(0, 0)
         quant_l(0)
-        stage1(1, 1, 0)
+        stage1(0, 0, 1)
+        load_cu(0)
+        quant_e(1, 0)
+        out_n(1, 0, S_COPY)
+        stage1(0, 1, 1)
+        mul_n(3, 0, nc.vector)
+        div_s(0, 0, 1)
+        turn_l(1, 1)
+        quant_n(1)
+        div_s(0, 1, 1)
+        stage1(0, 0, 0)
         quant_w("cu", 1, 0)
-        div_s(1, 1, 0)
-        turn_n(3, 1)
-        stage1(1, 0, 0)
-        mul_v(3, 0)
-        stage2_l(0, 0, 0)
-        mul_v(3, 1)
-        stage2_l(0, 0, 1)
-        inter("c", 1, 1, "s")
-        div_s(1, 0, 0)
-        stage1(1, 0, 1)
-        div_s(1, 0, 1)
-        turn_l(2, 1)
+        out_l(1, 0, S_COPY)
+        stage1(0, 1, 0)
+        load_c(1)
+        div_s(0, 0, 0)
+        div_s(0, 1, 0)
+        mul_n(2, 0, nc.gpsimd)
+        inter("cu", 0, 0, "s")
+        out_l(1, 1, S_COPY)
+        mul_n(2, 1, nc.vector)
+        quant_w("cu", 0, 0)
         turn_l(3, 1)
+        stage1(1, 0, 1)
+        out_l(3, 1, V_COPY)
         inter("c", 1, 0, "s")
-        stage1(1, 1, 1)
-        quant_l(1)
-        out_l(2, 1, S_COPY)
-        out_l(3, 1, S_COPY)
-        turn_l(3, 0)
-        quant_n(2)
-        turn_l(2, 0)
-        quant_j(0)
-        div_s(1, 1, 1)
-        stage1(2, 0, 0)
+        div_s(1, 0, 1)
+        turn_n(2, 0)
+        stage1(1, 0, 0)
+        mul_n(3, 1, nc.gpsimd)
+        stage2_l(0, 0, 1)
+        turn_n(3, 1)
         quant_w("c", 1, 0)
-        stage2_l(1, 0, 0)
-        quant_w("c", 0, 0)
-        inter("cu", 1, 1, "s")
+        stage1(1, 1, 0)
+        out_n(2, 0, S_COPY)
+        load_c(0)
+        out_n(3, 1, S_COPY)
+        turn_n(2, 1)
+        quant_l(1)
+        quant_j(0)
+        div_s(1, 0, 0)
+        turn_n(3, 0)
+        stage2_l(0, 0, 0)
+        out_n(2, 1, S_COPY)
         stage2_l(1, 0, 1)
-        div_s(2, 0, 0)
-        stage1(2, 0, 1)
-        stage2_j(0, 0, 1)
+        stage1(1, 1, 1)
+        stage2_l(1, 0, 0)
+        turn_l(3, 0)
+        out_n(3, 0, V_COPY)
+        quant_n(2)
+        inter("cu", 0, 1, "g")
+        load_l(2)
+        turn_l(2, 0)
+        inter("c", 0, 0, "s")
+        inter("c", 1, 1, "s")
+        div_s(1, 1, 0)
+        div_s(1, 1, 1)
+        quant_w("c", 0, 0)
         quant_j(1)
-        inter("c", 0, 1, "s")
-        stage2_j(0, 0, 0)
         stage1(2, 1, 0)
-        stage2_j(1, 0, 1)
-        stage2_j(1, 0, 0)
-        quant_w("cu", 1, 1)
-        div_s(2, 0, 1)
-        stage1(2, 1, 1)
-        quant_w("cu", 0, 1)
-        quant_w("c", 0, 1)
-        out_rows(0, 0, 0, S_COPY, True)
-        quant_w("c", 1, 1)
-        div_s(2, 1, 0)
-        out_rows(0, 0, 1, S_COPY)
-        stage2_l(1, 1, 0)
-        stage2_j(1, 1, 0)
-        stage2_l(0, 1, 0)
-        out_rows(1, 0, 0, S_COPY, True)
-        out_l(2, 0, V_COPY)
-        div_s(2, 1, 1)
-        stage2_j(0, 1, 0)
-        stage2_l(0, 1, 1)
-        out_l(3, 0, S_COPY)
-        out_rows(1, 0, 1, S_COPY, True)
-        stage2_l(1, 1, 1)
-        turn_p(1, 0)
-        turn_p(0, 0)
-        stage2_j(0, 1, 1)
-        out_p(1, 0, S_COPY)
         quant_n(3)
-        stage1(3, 1, 0)
-        out_rows(1, 1, 0, S_COPY)
-        div_s(3, 1, 0)
-        quant_l(2)
+        div_s(2, 1, 0)
+        stage1(2, 0, 0)
+        stage2_j(1, 0, 0)
+        stage2_j(1, 0, 1)
+        stage2_j(0, 0, 1)
         stage1(3, 0, 0)
-        out_rows(0, 1, 1, S_COPY, True)
-        stage2_j(1, 1, 1)
-        stage1(3, 0, 1)
-        out_rows(0, 1, 0, S_COPY, True)
-        out_p(0, 0, S_COPY)
+        div_s(2, 0, 0)
+        quant_w("c", 1, 1)
+        inter("cu", 1, 1, "g")
+        out_l(3, 0, S_COPY)
+        out_l(2, 0, V_COPY)
+        quant_w("cu", 0, 1)
+        out_rows(0, 0, 1, S_COPY)
+        stage2_j(0, 0, 0)
+        stage1(3, 1, 0)
         div_s(3, 0, 0)
-        quant_p(1, 0)
-        div_s(3, 0, 1)
-        stage2_l(2, 0, 0)
-        out_rows(1, 1, 1, S_COPY, True)
-        quant_j(2)
-        stage2_l(2, 1, 1)
-        stage2_l(2, 0, 1)
-        stage2_l(2, 1, 0)
-        turn_p(1, 1)
-        turn_p(0, 1)
-        stage2_j(2, 0, 0)
-        stage2_j(2, 1, 1)
-        out_p(0, 1, S_COPY)
-        quant_p(0, 0)
-        quant_l(3)
-        out_rows(2, 0, 0, V_COPY)
-        stage2_j(2, 1, 0)
-        stage2_j(2, 0, 1)
+        out_rows(0, 0, 0, S_COPY)
+        div_s(3, 1, 0)
+        turn_l(2, 1)
+        turn_p(0, 0)
+        stage1(2, 1, 1)
+        quant_w("cu", 1, 1)
+        stage1(2, 0, 1)
+        inter("c", 0, 1, "g")
+        out_rows(1, 0, 1, S_COPY)
+        stage2_l(0, 1, 0)
+        div_s(2, 1, 1)
+        stage1(3, 0, 1)
+        quant_w("c", 0, 1)
+        out_p(0, 0, V_COPY)
+        stage2_l(0, 1, 1)
+        div_s(2, 0, 1)
+        stage2_j(0, 1, 0)
+        stage2_l(1, 1, 0)
+        out_l(2, 1, S_COPY)
+        quant_l(2)
+        stage2_j(0, 1, 1)
+        out_rows(0, 1, 0, V_COPY)
+        stage2_j(1, 1, 0)
         stage1(3, 1, 1)
-        out_p(1, 1, V_COPY)
-        stage2_l(3, 0, 0)
-        out_rows(2, 1, 1, S_COPY)
-        quant_p(0, 1)
+        out_rows(1, 0, 0, S_COPY)
+        out_rows(1, 1, 0, V_COPY)
+        div_s(3, 0, 1)
+        out_rows(0, 1, 1, S_COPY, True)
+        stage2_l(1, 1, 1)
+        quant_p(0, 0)
+        turn_p(1, 0)
+        quant_j(2)
         div_s(3, 1, 1)
-        out_rows(2, 0, 1, S_COPY, True)
+        turn_p(0, 1)
+        stage2_l(2, 1, 0)
+        out_p(0, 1, S_COPY)
+        stage2_j(1, 1, 1)
+        stage2_l(2, 1, 1)
+        out_p(1, 0, S_COPY)
+        quant_l(3)
+        stage2_j(2, 1, 0)
+        out_rows(1, 1, 1, S_COPY)
+        stage2_j(2, 1, 1)
         out_rows(2, 1, 0, S_COPY)
+        stage2_l(2, 0, 0)
+        out_rows(2, 1, 1, S_COPY)
         quant_j(3)
-        stage2_l(3, 1, 1)
-        quant_p(1, 1)
+        stage2_j(2, 0, 0)
+        stage2_l(2, 0, 1)
+        quant_p(0, 1)
+        turn_p(1, 1)
         turn_p(2, 1)
-        turn_p(2, 0)
+        out_p(1, 1, V_COPY)
+        quant_p(1, 0)
+        quant_p(1, 1)
+        out_rows(2, 0, 0, S_COPY, True)
         out_p(2, 1, S_COPY)
+        stage2_j(2, 0, 1)
+        stage2_l(3, 1, 1)
+        out_rows(2, 0, 1, S_COPY, True)
         stage2_j(3, 1, 1)
-        stage2_l(3, 1, 0)
-        quant_p(2, 1)
-        stage2_j(3, 0, 0)
-        out_p(2, 0, S_COPY)
-        quant_p(2, 0)
-        stage2_l(3, 0, 1)
+        turn_p(2, 0)
         out_rows(3, 1, 1, S_COPY, True)
-        stage2_j(3, 0, 1)
-        out_rows(3, 0, 0, S_COPY, True)
-        store_scales(0, ROWS * 3)
-        out_rows(3, 0, 1, V_COPY)
+        out_p(2, 0, V_COPY)
+        stage2_l(3, 1, 0)
+        quant_p(2, 0)
         stage2_j(3, 1, 0)
-        turn_p(3, 0)
         out_rows(3, 1, 0, S_COPY, True)
+        quant_p(2, 1)
+        stage2_l(3, 0, 0)
+        stage2_l(3, 0, 1)
+        stage2_j(3, 0, 0)
+        store_scales(0, ROWS * 3)
+        out_rows(3, 0, 0, V_COPY)
+        stage2_j(3, 0, 1)
+        out_rows(3, 0, 1, S_COPY, True)
         turn_p(3, 1)
-        out_p(3, 0, S_COPY)
         out_p(3, 1, S_COPY)
-        quant_p(3, 0)
+        turn_p(3, 0)
         quant_p(3, 1)
+        out_p(3, 0, S_COPY)
+        quant_p(3, 0)
         store_scales(ROWS * 3, D)

@@ -49,8 +49,8 @@ def tile_relativefluctuationcovariancedrift_kernel(tc, n, v, a, s, c, l, cu, out
 
         for g in range(2):
             nc.sync.dma_start(
-                out=srow[4 * g : 4 * g + 4, :].rearrange("t (b q) -> t b q", q=8),
-                in_=s[512 * g : 512 * g + 512].rearrange("(b t q) -> t b q", t=4, q=8),
+                out=srow[4 * g : 4 * g + 4, :].rearrange("t (y i) -> t y i", i=4),
+                in_=s[512 * g : 512 * g + 512].rearrange("(y t i) -> t y i", t=4, i=4),
             )
         nc.sync.dma_start(out=srow[8:16, :], in_=s.rearrange("(x p) -> x p", p=P))
         nc.sync.dma_start(out=srow[16:24, :], in_=v.rearrange("(x p) -> x p", p=P))
@@ -78,7 +78,7 @@ def tile_relativefluctuationcovariancedrift_kernel(tc, n, v, a, s, c, l, cu, out
             nc.sync.dma_start(out=raw[g][:], in_=src[512 * g : 512 * g + 512, :].rearrange("(p j) w -> p j w", j=4))
 
         def load_c(g):
-            rows = c[512 * g : 512 * g + 512, :].rearrange("(b t q) z -> t b q z", t=4, q=8)
+            rows = c[512 * g : 512 * g + 512, :].rearrange("(y t i) z -> t y i z", t=4, i=4)
             for t in range(4):
                 nc.sync.dma_start(out=c_raw[g][:, t, :], in_=rows[t])
 
@@ -204,11 +204,11 @@ def tile_relativefluctuationcovariancedrift_kernel(tc, n, v, a, s, c, l, cu, out
             if (g, G) not in eps_bf:
                 eps_bf[g, G] = wt("eps_bf", [P, 4, P, 4], BF16, 3)
             e_t = e_row[G][:, t] if on_gpsimd else e_ps[G][:, t]
-            out = eps_bf[g, G][:, t].rearrange("p (b q) j -> p b q j", q=8)
-            in0 = a_raw[g][:, :, 512 * G : 512 * G + 512].rearrange("p j (b t q) -> p t b q j", t=4, q=8)[:, t]
-            in1 = e_t.rearrange("p (b q) -> p b q", q=8).unsqueeze(3).to_broadcast([P, 16, 8, 4])
+            out = eps_bf[g, G][:, t].rearrange("p (y i) j -> p y j i", i=4)
+            in0 = a_raw[g][:, :, 512 * G : 512 * G + 512].rearrange("p j (y t i) -> p t y j i", t=4, i=4)[:, t]
+            in1 = e_t.rearrange("p (y i) -> p y i", i=4).unsqueeze(2).to_broadcast([P, 32, 4, 4])
             if on_gpsimd:
-                for b in (slice(0, 8), slice(8, 16)):
+                for b in (slice(0, 16), slice(16, 32)):
                     nc.gpsimd.tensor_tensor(out=out[:, b], in0=in0[:, b], in1=in1[:, b], op=MULT)
             else:
                 nc.vector.tensor_tensor(out=out, in0=in0, in1=in1, op=MULT)
@@ -378,218 +378,216 @@ def tile_relativefluctuationcovariancedrift_kernel(tc, n, v, a, s, c, l, cu, out
 
         S_COPY, V_COPY = nc.scalar.copy, nc.vector.tensor_copy
         T4 = range(4)
-        load_a(1)
-        spread_e(1)
         spread_e(0)
-        keep_e(1)
-        load_a(0)
-        load_l(0)
-        load_n(0)
-        mul_e(1, 1, 0)
-        mul_e(1, 1, 2)
-        load_n(1)
-        mul_e(1, 1, 1, True)
-        mul_e(1, 1, 3)
-        load_cu(1)
-        mul_e(0, 1, 2)
-        keep_e(0)
-        quant_e(1, 1)
-        spread_v()
-        mul_e(0, 1, 1)
-        mul_e(0, 1, 3, True)
-        mul_e(1, 0, 3)
-        load_l(1)
+        load_a(1)
         mul_e(1, 0, 0)
-        mul_n(0, 1, nc.vector)
-        mul_n(0, 0, nc.vector)
+        load_a(0)
+        load_cu(1)
+        spread_e(1)
+        mul_e(1, 0, 2)
+        spread_v()
+        load_l(0)
+        mul_e(1, 1, 0)
+        inter("cu", 1, 1, "s")
+        mul_e(1, 0, 3)
+        mul_e(1, 1, 1)
+        load_n(0)
+        mul_e(1, 1, 2)
         mul_e(1, 0, 1)
-        mul_e(0, 1, 0, True)
-        load_n(2)
-        spread_rs(1)
-        load_n(3)
-        spread_rs(0)
-        mul_n(1, 1, nc.vector)
-        turn_l(0, 1)
-        turn_l(0, 0)
-        out_l(0, 1, S_COPY)
-        mul_e(0, 0, 2, True)
-        turn_n(0, 1)
-        mul_n(1, 0, nc.vector)
-        mul_e(0, 0, 3)
-        quant_e(0, 1)
-        out_l(0, 0, S_COPY)
-        out_n(0, 1, S_COPY)
-        turn_n(0, 0)
-        mul_e(1, 0, 2, True)
-        turn_n(1, 1)
-        out_n(0, 0, S_COPY)
-        load_l(3)
-        out_n(1, 1, S_COPY)
-        mul_e(0, 0, 1)
-        turn_n(1, 0)
-        inter("cu", 1, 0, "s")
-        mul_e(0, 0, 0, True)
-        quant_n(0)
-        turn_l(1, 0)
-        quant_e(0, 0)
-        quant_l(0)
-        stage1(0, 0, 1)
-        load_cu(0)
+        mul_e(0, 0, 0)
         quant_e(1, 0)
+        load_n(1)
+        spread_rs(0)
+        load_l(1)
+        mul_e(0, 0, 3)
+        mul_e(0, 1, 2)
+        mul_e(0, 0, 1)
+        load_n(3)
+        mul_n(0, 0, nc.vector)
+        turn_l(0, 1)
+        mul_n(0, 1, nc.vector)
+        out_l(0, 1, S_COPY)
+        turn_l(0, 0)
+        mul_n(1, 1, nc.vector)
+        out_l(0, 0, S_COPY)
+        spread_rs(1)
+        load_l(2)
+        mul_n(1, 0, nc.vector)
+        mul_e(0, 1, 3)
+        mul_e(0, 0, 2)
+        turn_n(0, 0)
+        out_n(0, 0, S_COPY)
+        load_cu(0)
+        turn_n(0, 1)
+        turn_n(1, 1)
+        out_n(0, 1, S_COPY)
+        inter("cu", 1, 0, "s")
+        out_n(1, 1, S_COPY)
+        quant_l(0)
+        quant_e(0, 0)
+        turn_n(1, 0)
+        quant_n(0)
+        load_n(2)
+        mul_n(3, 1, nc.vector)
         out_n(1, 0, S_COPY)
-        stage1(0, 1, 1)
+        mul_e(1, 1, 3)
+        turn_l(1, 0)
+        mul_e(0, 1, 1)
+        mul_e(0, 1, 0)
         mul_n(3, 0, nc.vector)
-        div_s(0, 0, 1)
-        turn_l(1, 1)
-        quant_n(1)
-        div_s(0, 1, 1)
-        stage1(0, 0, 0)
-        quant_w("cu", 1, 0)
-        out_l(1, 0, S_COPY)
+        quant_e(0, 1)
+        inter("cu", 0, 0, "s")
         stage1(0, 1, 0)
         load_c(1)
-        div_s(0, 0, 0)
+        out_l(1, 0, S_COPY)
+        quant_e(1, 1)
+        turn_l(1, 1)
+        stage1(0, 0, 0)
         div_s(0, 1, 0)
-        mul_n(2, 0, nc.gpsimd)
-        inter("cu", 0, 0, "s")
-        out_l(1, 1, S_COPY)
-        mul_n(2, 1, nc.vector)
-        quant_w("cu", 0, 0)
-        turn_l(3, 1)
-        stage1(1, 0, 1)
-        out_l(3, 1, V_COPY)
-        inter("c", 1, 0, "s")
-        div_s(1, 0, 1)
-        turn_n(2, 0)
-        stage1(1, 0, 0)
-        mul_n(3, 1, nc.gpsimd)
-        stage2_l(0, 0, 1)
-        turn_n(3, 1)
-        quant_w("c", 1, 0)
-        stage1(1, 1, 0)
-        out_n(2, 0, S_COPY)
+        div_s(0, 0, 0)
+        quant_n(1)
+        stage1(0, 0, 1)
         load_c(0)
-        out_n(3, 1, S_COPY)
-        turn_n(2, 1)
-        quant_l(1)
-        quant_j(0)
-        div_s(1, 0, 0)
-        turn_n(3, 0)
-        stage2_l(0, 0, 0)
-        out_n(2, 1, S_COPY)
-        stage2_l(1, 0, 1)
-        stage1(1, 1, 1)
-        stage2_l(1, 0, 0)
-        turn_l(3, 0)
-        out_n(3, 0, V_COPY)
-        quant_n(2)
-        inter("cu", 0, 1, "g")
-        load_l(2)
-        turn_l(2, 0)
-        inter("c", 0, 0, "s")
-        inter("c", 1, 1, "s")
-        div_s(1, 1, 0)
-        div_s(1, 1, 1)
-        quant_w("c", 0, 0)
-        quant_j(1)
-        stage1(2, 1, 0)
-        quant_n(3)
-        div_s(2, 1, 0)
-        stage1(2, 0, 0)
-        stage2_j(1, 0, 0)
-        stage2_j(1, 0, 1)
-        stage2_j(0, 0, 1)
-        stage1(3, 0, 0)
-        div_s(2, 0, 0)
-        quant_w("c", 1, 1)
-        inter("cu", 1, 1, "g")
-        out_l(3, 0, S_COPY)
-        out_l(2, 0, V_COPY)
-        quant_w("cu", 0, 1)
-        out_rows(0, 0, 1, S_COPY)
-        stage2_j(0, 0, 0)
-        stage1(3, 1, 0)
-        div_s(3, 0, 0)
-        out_rows(0, 0, 0, S_COPY)
-        div_s(3, 1, 0)
+        stage1(0, 1, 1)
+        turn_n(3, 1)
+        quant_w("cu", 0, 0)
+        out_l(1, 1, S_COPY)
+        inter("c", 1, 0, "s")
+        quant_w("cu", 1, 0)
         turn_l(2, 1)
-        turn_p(0, 0)
-        stage1(2, 1, 1)
-        quant_w("cu", 1, 1)
-        stage1(2, 0, 1)
-        inter("c", 0, 1, "g")
-        out_rows(1, 0, 1, S_COPY)
-        stage2_l(0, 1, 0)
-        div_s(2, 1, 1)
-        stage1(3, 0, 1)
-        quant_w("c", 0, 1)
-        out_p(0, 0, V_COPY)
-        stage2_l(0, 1, 1)
-        div_s(2, 0, 1)
-        stage2_j(0, 1, 0)
-        stage2_l(1, 1, 0)
+        stage2_l(0, 0, 1)
+        out_n(3, 1, S_COPY)
+        div_s(0, 0, 1)
+        div_s(0, 1, 1)
+        mul_n(2, 0, nc.vector)
         out_l(2, 1, S_COPY)
-        quant_l(2)
-        stage2_j(0, 1, 1)
-        out_rows(0, 1, 0, V_COPY)
-        stage2_j(1, 1, 0)
-        stage1(3, 1, 1)
+        stage2_l(0, 0, 0)
+        stage1(1, 0, 0)
+        stage1(1, 1, 0)
+        mul_n(2, 1, nc.vector)
+        quant_l(1)
+        load_l(3)
+        div_s(1, 0, 0)
+        turn_n(2, 0)
+        div_s(1, 1, 0)
+        quant_w("c", 1, 0)
+        turn_n(2, 1)
+        inter("c", 0, 0, "s")
+        stage2_l(1, 0, 0)
+        quant_w("c", 0, 0)
+        stage2_l(1, 0, 1)
+        quant_j(0)
+        stage1(1, 0, 1)
+        stage1(1, 1, 1)
+        out_n(2, 0, S_COPY)
+        out_n(2, 1, S_COPY)
+        inter("c", 1, 1, "s")
+        turn_n(3, 0)
+        div_s(1, 0, 1)
+        turn_l(3, 0)
+        stage2_j(0, 0, 0)
+        quant_n(2)
+        stage2_j(0, 0, 1)
+        div_s(1, 1, 1)
+        quant_j(1)
+        stage1(2, 0, 1)
+        quant_w("cu", 1, 1)
+        stage1(2, 1, 0)
+        stage2_j(1, 0, 0)
+        div_s(2, 0, 1)
+        inter("cu", 0, 1, "v")
+        div_s(2, 1, 0)
+        out_l(3, 0, S_COPY)
+        quant_w("cu", 0, 1)
+        quant_w("c", 1, 1)
+        out_n(3, 0, S_COPY)
+        out_rows(0, 0, 1, S_COPY, True)
+        inter("c", 0, 1, "s")
+        out_rows(0, 0, 0, S_COPY)
         out_rows(1, 0, 0, S_COPY)
-        out_rows(1, 1, 0, V_COPY)
-        div_s(3, 0, 1)
-        out_rows(0, 1, 1, S_COPY, True)
+        quant_w("c", 0, 1)
+        stage2_j(1, 0, 1)
+        turn_l(2, 0)
+        turn_l(3, 1)
+        stage1(2, 1, 1)
+        out_l(2, 0, V_COPY)
+        stage1(2, 0, 0)
         stage2_l(1, 1, 1)
-        quant_p(0, 0)
-        turn_p(1, 0)
-        quant_j(2)
-        div_s(3, 1, 1)
-        turn_p(0, 1)
-        stage2_l(2, 1, 0)
-        out_p(0, 1, S_COPY)
+        quant_n(3)
+        stage2_l(0, 1, 1)
+        stage2_l(0, 1, 0)
+        out_rows(1, 0, 1, S_COPY, True)
+        div_s(2, 1, 1)
         stage2_j(1, 1, 1)
-        stage2_l(2, 1, 1)
-        out_p(1, 0, S_COPY)
-        quant_l(3)
-        stage2_j(2, 1, 0)
+        quant_l(2)
+        stage2_l(1, 1, 0)
+        stage2_j(0, 1, 1)
+        div_s(2, 0, 0)
+        stage2_j(0, 1, 0)
+        stage1(3, 1, 0)
+        out_l(3, 1, S_COPY)
+        turn_p(1, 0)
+        turn_p(0, 0)
         out_rows(1, 1, 1, S_COPY)
-        stage2_j(2, 1, 1)
-        out_rows(2, 1, 0, S_COPY)
+        out_rows(0, 1, 1, V_COPY)
         stage2_l(2, 0, 0)
-        out_rows(2, 1, 1, S_COPY)
-        quant_j(3)
+        quant_j(2)
+        out_rows(0, 1, 0, S_COPY, True)
+        stage1(3, 0, 1)
+        out_p(1, 0, S_COPY)
+        out_p(0, 0, S_COPY)
+        quant_p(0, 0)
+        stage2_j(1, 1, 0)
+        div_s(3, 1, 0)
         stage2_j(2, 0, 0)
         stage2_l(2, 0, 1)
-        quant_p(0, 1)
-        turn_p(1, 1)
-        turn_p(2, 1)
-        out_p(1, 1, V_COPY)
-        quant_p(1, 0)
-        quant_p(1, 1)
-        out_rows(2, 0, 0, S_COPY, True)
-        out_p(2, 1, S_COPY)
         stage2_j(2, 0, 1)
-        stage2_l(3, 1, 1)
-        out_rows(2, 0, 1, S_COPY, True)
-        stage2_j(3, 1, 1)
-        turn_p(2, 0)
-        out_rows(3, 1, 1, S_COPY, True)
-        out_p(2, 0, V_COPY)
-        stage2_l(3, 1, 0)
-        quant_p(2, 0)
-        stage2_j(3, 1, 0)
-        out_rows(3, 1, 0, S_COPY, True)
-        quant_p(2, 1)
+        div_s(3, 0, 1)
+        stage1(3, 0, 0)
+        out_rows(2, 0, 0, S_COPY, True)
+        stage2_l(2, 1, 1)
+        out_rows(1, 1, 0, S_COPY)
+        stage1(3, 1, 1)
+        turn_p(1, 1)
+        quant_l(3)
+        turn_p(0, 1)
+        div_s(3, 0, 0)
+        div_s(3, 1, 1)
+        quant_p(1, 0)
+        quant_j(3)
+        out_rows(2, 0, 1, S_COPY)
+        stage2_l(2, 1, 0)
+        stage2_j(2, 1, 1)
         stage2_l(3, 0, 0)
-        stage2_l(3, 0, 1)
+        out_p(1, 1, S_COPY)
+        stage2_l(3, 1, 0)
+        stage2_j(2, 1, 0)
+        out_p(0, 1, S_COPY)
+        out_rows(2, 1, 1, S_COPY)
+        quant_p(1, 1)
+        out_rows(2, 1, 0, S_COPY, True)
+        stage2_j(3, 1, 0)
         stage2_j(3, 0, 0)
-        store_scales(0, ROWS * 3)
-        out_rows(3, 0, 0, V_COPY)
+        quant_p(0, 1)
+        turn_p(2, 1)
+        turn_p(2, 0)
+        out_rows(3, 1, 0, S_COPY, True)
+        out_p(2, 0, V_COPY)
+        stage2_l(3, 0, 1)
+        out_p(2, 1, S_COPY)
+        quant_p(2, 1)
+        out_rows(3, 0, 0, S_COPY, True)
+        quant_p(2, 0)
         stage2_j(3, 0, 1)
+        store_scales(0, ROWS * 3)
+        stage2_l(3, 1, 1)
+        stage2_j(3, 1, 1)
         out_rows(3, 0, 1, S_COPY, True)
-        turn_p(3, 1)
-        out_p(3, 1, S_COPY)
+        out_rows(3, 1, 1, S_COPY)
         turn_p(3, 0)
-        quant_p(3, 1)
-        out_p(3, 0, S_COPY)
+        turn_p(3, 1)
+        out_p(3, 0, V_COPY)
         quant_p(3, 0)
+        out_p(3, 1, S_COPY)
+        quant_p(3, 1)
         store_scales(ROWS * 3, D)

@@ -3,8 +3,8 @@ from contextlib import ExitStack
 import concourse.mybir as mybir
 from concourse.masks import make_identity
 
-D = 1024
-FLOPS = 3 * 2 * D * D * D
+N = 1024
+FLOPS = 3 * 2 * N * N * N
 
 F32 = mybir.dt.float32
 BF16 = mybir.dt.bfloat16
@@ -16,578 +16,551 @@ MULT = mybir.AluOpType.mult
 ADD = mybir.AluOpType.add
 
 P = 128
-SB = 4
+PASS = 512
 ROWS = 256
-TRB = 2
-S1B = 2
-S2B = 4
+SUPERBLOCKS = N // ROWS
+
+TURN_BANKS = 3
+K_BANKS = 2
+ROW_BANKS = 3
 
 
 def tile_relativefluctuationcovariancedrift_kernel(tc, n, v, a, s, c, l, cu, out_0, out_1, out_2):
     nc = tc.nc
+    by_vector = nc.vector.tensor_copy
+    by_scalar = nc.scalar.copy
+
     with ExitStack() as ctx:
         keep = ctx.enter_context(tc.tile_pool(name="keep", bufs=1))
-        work = ctx.enter_context(tc.tile_pool(name="work", bufs=2))
+        work = ctx.enter_context(tc.tile_pool(name="work", bufs=1))
         psum = ctx.enter_context(tc.psum_pool(name="psum", bufs=1))
         ctx.enter_context(tc.manual_schedule())
 
-        def kt(name, shape, dtype):
+        def kept(name, shape, dtype):
             return keep.tile(shape, dtype, name=name, tag=name, align_bytes=64)
 
-        def wt(tag, shape, dtype, bufs):
+        def rotating(tag, shape, dtype, bufs):
             return work.tile(shape, dtype, name=tag, tag=tag, bufs=bufs, align_bytes=64)
 
-        def bank(tag, shape, dtype, bufs):
-            return psum.tile(shape, dtype, name=tag, tag=tag, bufs=bufs)
+        def turn_bank(shape, dtype=F32):
+            return psum.tile(shape, dtype, name="turn_bank", tag="turn_bank", bufs=TURN_BANKS)
 
-        srow = kt("srow", [P, P], BF16)
-        nc.vector.memset(srow[:], 0.0)
-        ident = kt("ident", [P, P], F32)
-        make_identity(nc, ident[:])
-        identb = kt("identb", [P, P], BF16)
-        nc.vector.tensor_copy(out=identb[:], in_=ident[:])
+        def k_bank():
+            return psum.tile([P, 4, P], F32, name="k_bank", tag="k_bank", bufs=K_BANKS)
 
-        for g in range(2):
-            nc.sync.dma_start(
-                out=srow[4 * g : 4 * g + 4, :].rearrange("t (y i) -> t y i", i=4),
-                in_=s[512 * g : 512 * g + 512].rearrange("(y t i) -> t y i", t=4, i=4),
+        def row_bank(shape):
+            return psum.tile(shape, F32, name="row_bank", tag="row_bank", bufs=ROW_BANKS)
+
+        def quantize(codes, scales, values):
+            nc.vector.quantize_mx(out=codes.bitcast(FP8X4), scales=scales, in_=values)
+
+        def multiply(out, stationary, moving, start, stop):
+            nc.tensor.matmul_mx(
+                out=out,
+                lhsT=stationary[0].bitcast(FP8X4),
+                lhsT_scale=stationary[1],
+                rhs=moving[0].bitcast(FP8X4),
+                rhs_scale=moving[1],
+                start=start,
+                stop=stop,
             )
-        nc.sync.dma_start(out=srow[8:16, :], in_=s.rearrange("(x p) -> x p", p=P))
-        nc.sync.dma_start(out=srow[16:24, :], in_=v.rearrange("(x p) -> x p", p=P))
 
-        n_raw, l_raw = {}, {}
-        a_raw = [kt("a_raw%d" % g, [P, 4, D], BF16) for g in range(2)]
-        cu_raw = [kt("cu_raw%d" % g, [P, 4, D], BF16) for g in range(2)]
-        c_raw = [kt("c_raw%d" % g, [P, 4, D], BF16) for g in range(2)]
+        vector_rows = kept("vector_rows", [P, P], BF16)
+        nc.vector.memset(vector_rows[:], 0.0)
+        identity = kept("identity", [P, P], F32)
+        make_identity(nc, identity[:])
+        identity_bf16 = kept("identity_bf16", [P, P], BF16)
+        nc.vector.tensor_copy(out=identity_bf16[:], in_=identity[:])
 
-        def load_n(k):
-            n_raw[k] = wt("n_raw", [P, 2, D], BF16, 3)
-            nc.sync.dma_start(out=n_raw[k][:], in_=n[ROWS * k : ROWS * k + ROWS, :].rearrange("(b p) r -> p b r", p=P))
+        for G in range(2):
+            nc.sync.dma_start(
+                out=vector_rows[4 * G : 4 * G + 4, :].rearrange("t (y i) -> t y i", i=4),
+                in_=s[PASS * G : PASS * G + PASS].rearrange("(y t i) -> t y i", t=4, i=4),
+            )
+        nc.sync.dma_start(out=vector_rows[8:16, :], in_=s.rearrange("(x p) -> x p", p=P))
+        nc.sync.dma_start(out=vector_rows[16:24, :], in_=v.rearrange("(x p) -> x p", p=P))
 
-        def load_l(k):
-            l_raw[k] = wt("l_raw", [P, 2, D], BF16, 3)
-            nc.sync.dma_start(out=l_raw[k][:], in_=l[ROWS * k : ROWS * k + ROWS, :].rearrange("(b p) r -> p b r", p=P))
+        columns = turn_bank([P, P], BF16)
+        nc.tensor.transpose(columns[:], vector_rows[:], identity_bf16[:])
+        s_cols = kept("s_cols", [P, 16], F32)
+        nc.vector.tensor_copy(out=s_cols[:], in_=columns[:, 0:16])
+        s_squared = kept("s_squared", [P, 8], F32)
+        nc.vector.tensor_tensor(out=s_squared[:], in0=s_cols[:, 0:8], in1=s_cols[:, 0:8], op=MULT)
+        half_sum = kept("half_sum", [P, 8], F32)
+        nc.vector.tensor_scalar(out=half_sum[:], in0=s_squared[:], scalar1=0.5, scalar2=0.5, op0=MULT, op1=ADD)
+        e_cols = kept("e_cols", [P, 8], F32)
+        nc.vector.reciprocal(out=e_cols[:], in_=half_sum[:])
+        inv_s_cols = kept("inv_s_cols", [P, 8], F32)
+        nc.vector.reciprocal(out=inv_s_cols[:], in_=s_cols[:, 8:16])
+        v_cols = kept("v_cols", [P, 8], BF16)
+        nc.vector.tensor_copy(out=v_cols[:], in_=columns[:, 16:24])
 
-        def load_a(g):
-            load_w(a_raw, a, g)
-
-        def load_cu(g):
-            load_w(cu_raw, cu, g)
-
-        def load_w(raw, src, g):
-            nc.sync.dma_start(out=raw[g][:], in_=src[512 * g : 512 * g + 512, :].rearrange("(p j) w -> p j w", j=4))
-
-        def load_c(g):
-            rows = c[512 * g : 512 * g + 512, :].rearrange("(y t i) z -> t y i z", t=4, i=4)
-            for t in range(4):
-                nc.sync.dma_start(out=c_raw[g][:, t, :], in_=rows[t])
-
-
-        s_ps = bank("tr", [P, P], BF16, TRB)
-        nc.tensor.transpose(s_ps[:], srow[:], identb[:])
-        s_cols = kt("s_cols", [P, 16], F32)
-        nc.vector.tensor_copy(out=s_cols[:], in_=s_ps[:, 0:16])
-        s_sq = kt("s_sq", [P, 8], F32)
-        nc.vector.tensor_tensor(out=s_sq[:], in0=s_cols[:, 0:8], in1=s_cols[:, 0:8], op=MULT)
-        s_half = kt("s_half", [P, 8], F32)
-        nc.vector.tensor_scalar(out=s_half[:], in0=s_sq[:], scalar1=0.5, scalar2=0.5, op0=MULT, op1=ADD)
-        e4 = kt("e4", [P, 8], F32)
-        nc.vector.reciprocal(out=e4[:], in_=s_half[:])
-        rs8 = kt("rs8", [P, 8], F32)
-        nc.vector.reciprocal(out=rs8[:], in_=s_cols[:, 8:16])
-
-        v_cols = kt("v_cols", [P, 8], BF16)
-        nc.vector.tensor_copy(out=v_cols[:], in_=s_ps[:, 16:24])
-        v_row = kt("v_row", [P, D], BF16)
+        v_row = kept("v_row", [P, N], BF16)
+        inv_s_row = kept("inv_s_row", [P, N], F32)
+        e_banks = {}
 
         def spread_v():
-            b = bank("tr", [P, 8, P], BF16, TRB)
+            b = turn_bank([P, 8, P], BF16)
             for x in range(8):
-                nc.tensor.transpose(b[:, x, :], v_cols[:, x : x + 1].to_broadcast([P, P]), identb[:])
-            nc.scalar.copy(out=v_row[:], in_=b[:].rearrange("p x i -> p (x i)"))
+                nc.tensor.transpose(b[:, x, :], v_cols[:, x : x + 1].to_broadcast([P, P]), identity_bf16[:])
+            nc.scalar.copy(out=v_row[:], in_=b[:].rearrange("p x r -> p (x r)"))
 
-        e_ps = {}
+        def spread_inv_s(half):
+            b = k_bank()
+            for x in range(4):
+                col = 4 * half + x
+                nc.tensor.transpose(b[:, x, :], inv_s_cols[:, col : col + 1].to_broadcast([P, P]), identity[:])
+            nc.scalar.copy(out=inv_s_row[:, PASS * half : PASS * half + PASS], in_=b[:].rearrange("p x i -> p (x i)"))
 
         def spread_e(G):
-            e_ps[G] = bank("s2", [P, 4, P], F32, S2B)
+            e_banks[G] = row_bank([P, 4, P])
             for t in range(4):
-                j = 4 * G + t
-                nc.tensor.transpose(e_ps[G][:, t, :], e4[:, j : j + 1].to_broadcast([P, P]), ident[:])
+                col = 4 * G + t
+                nc.tensor.transpose(e_banks[G][:, t, :], e_cols[:, col : col + 1].to_broadcast([P, P]), identity[:])
 
-        rs_row = kt("rs_row", [P, D], F32)
+        a_raw = [kept("a_raw%d" % g, [P, 4, N], BF16) for g in range(2)]
+        cu_raw = [kept("cu_raw%d" % g, [P, 4, N], BF16) for g in range(2)]
+        c_raw = [kept("c_raw%d" % G, [P, 4, N], BF16) for G in range(2)]
+        n_raw, l_raw = {}, {}
+        whole = slice(0, N)
+        halves = [slice(0, PASS), slice(PASS, N)]
 
-        def spread_rs(y):
-            b = bank("s1", [P, 4, P], F32, S1B)
-            for x in range(4):
-                nc.tensor.transpose(b[:, x, :], rs8[:, 4 * y + x : 4 * y + x + 1].to_broadcast([P, P]), ident[:])
-            nc.scalar.copy(out=rs_row[:, 512 * y : 512 * y + 512], in_=b[:].rearrange("p x i -> p (x i)"))
+        def load_grouped(raw, source, g, cols):
+            rows = source[PASS * g : PASS * g + PASS, cols]
+            nc.sync.dma_start(out=raw[g][:, :, cols], in_=rows.rearrange("(p j) w -> p j w", j=4))
 
-        tr_ps = {}
+        def load_c(G):
+            rows = c[PASS * G : PASS * G + PASS, :].rearrange("(y t i) z -> t y i z", t=4, i=4)
+            for t in range(4):
+                nc.sync.dma_start(out=c_raw[G][:, t, :], in_=rows[t])
 
-        def turn_l(k, g):
-            b = bank("tr", [P, 2, 2, P], F32, TRB)
-            words = l_raw[k][:].bitcast(F32)
-            for u in range(2):
-                for ib in range(2):
-                    nc.tensor.transpose(b[:, u, ib, :], words[:, ib, 256 * g + u : 256 * g + 256 : 2], ident[:])
-            tr_ps["l", k, g] = b
+        def load_rows(raw, source, k):
+            tag = "n_raw" if raw is n_raw else "l_raw"
+            raw[k] = rotating(tag, [P, 2, N], BF16, 3)
+            rows = source[ROWS * k : ROWS * k + ROWS, :]
+            nc.sync.dma_start(out=raw[k][:], in_=rows.rearrange("(b p) r -> p b r", p=P))
 
-        nv, n_bf, n_codes, n_scales = {}, {}, {}, {}
-        l_bf, l_codes, l_scales = {}, {}, {}
+        nv, turned = {}, {}
+        n_op = {"tag": "n_bf", "bufs": 2, "values": {}, "codes": {}, "scales": {}}
+        l_op = {"tag": "l_bf", "bufs": 3, "values": {}, "codes": {}, "scales": {}}
 
-        def mul_n(k, ib, eng):
+        def scale_n(k, w):
             if k not in nv:
-                nv[k] = wt("nv", [P, 2, D], BF16, 2)
-            for g in range(2):
-                cols = slice(512 * g, 512 * g + 512)
-                eng.tensor_tensor(
-                    out=nv[k][:, ib, cols].rearrange("p (u m e) -> p u m e", u=2, e=2),
-                    in0=n_raw[k][:, ib, cols].rearrange("p (m u e) -> p u m e", u=2, e=2),
-                    in1=v_row[:, cols].rearrange("p (m u e) -> p u m e", u=2, e=2),
-                    op=MULT,
-                )
-
-        def turn_n(k, g):
-            b = bank("tr", [P, 2, 2, P], F32, TRB)
-            words = nv[k][:].bitcast(F32)
-            for u in range(2):
-                for ib in range(2):
-                    w0 = 256 * g + 128 * u
-                    nc.tensor.transpose(b[:, u, ib, :], words[:, ib, w0 : w0 + 128], ident[:])
-            tr_ps["n", k, g] = b
-
-        def out_n(k, g, copy):
-            if k not in n_bf:
-                n_bf[k] = wt("n_bf", [P, 2, ROWS, 4], BF16, 2)
-            b = tr_ps.pop(("n", k, g))
-            copy(
-                out=n_bf[k][:, g].rearrange("p i t -> p (i t)").bitcast(F32).rearrange("p (i u) -> p i u", u=2),
-                in_=b[:].rearrange("p u b i -> p (b i) u"),
-            )
-
-        def quant_n(k):
-            n_codes[k] = kt("n_codes%d" % k, [P, 2, ROWS], U32)
-            n_scales[k] = kt("n_scales%d" % k, [P, 2, ROWS], U8)
-            nc.vector.quantize_mx(
-                out=n_codes[k][:].rearrange("p g i -> p (g i)").bitcast(FP8X4),
-                scales=n_scales[k][:].rearrange("p g i -> p (g i)"),
-                in_=n_bf[k][:].rearrange("p g i t -> p (g i t)"),
-            )
-
-        def out_l(k, g, copy):
-            if k not in l_bf:
-                l_bf[k] = wt("l_bf", [P, 2, ROWS, 4], BF16, 3)
-            b = tr_ps.pop(("l", k, g))
-            copy(
-                out=l_bf[k][:, g].rearrange("p i t -> p (i t)").bitcast(F32).rearrange("p (i u) -> p i u", u=2),
-                in_=b[:].rearrange("p u b i -> p (b i) u"),
-            )
-
-        def quant_l(k):
-            l_codes[k] = kt("l_codes%d" % k, [P, 2, ROWS], U32)
-            l_scales[k] = kt("l_scales%d" % k, [P, 2, ROWS], U8)
-            nc.vector.quantize_mx(
-                out=l_codes[k][:].rearrange("p g i -> p (g i)").bitcast(FP8X4),
-                scales=l_scales[k][:].rearrange("p g i -> p (g i)"),
-                in_=l_bf[k][:].rearrange("p g i t -> p (g i t)"),
-            )
-
-        eps_bf, eps_codes, eps_scales = {}, {}, {}
-
-        e_row = {}
-
-        def keep_e(G):
-            e_row[G] = kt("e_row%d" % G, [P, 4, P], F32)
-            nc.scalar.copy(out=e_row[G][:].rearrange("p t m -> p (t m)"), in_=e_ps[G][:].rearrange("p t m -> p (t m)"))
-
-        def mul_e(g, G, t, on_gpsimd=False):
-            if (g, G) not in eps_bf:
-                eps_bf[g, G] = wt("eps_bf", [P, 4, P, 4], BF16, 3)
-            e_t = e_row[G][:, t] if on_gpsimd else e_ps[G][:, t]
-            out = eps_bf[g, G][:, t].rearrange("p (y i) j -> p y j i", i=4)
-            in0 = a_raw[g][:, :, 512 * G : 512 * G + 512].rearrange("p j (y t i) -> p t y j i", t=4, i=4)[:, t]
-            in1 = e_t.rearrange("p (y i) -> p y i", i=4).unsqueeze(2).to_broadcast([P, 32, 4, 4])
-            if on_gpsimd:
-                for b in (slice(0, 16), slice(16, 32)):
-                    nc.gpsimd.tensor_tensor(out=out[:, b], in0=in0[:, b], in1=in1[:, b], op=MULT)
-            else:
-                nc.vector.tensor_tensor(out=out, in0=in0, in1=in1, op=MULT)
-
-        def quant_e(g, G):
-            eps_codes[g, G] = kt("eps_codes%d%d" % (g, G), [P, 512], U32)
-            eps_scales[g, G] = kt("eps_scales%d%d" % (g, G), [P, 512], U8)
-            nc.vector.quantize_mx(
-                out=eps_codes[g, G][:].bitcast(FP8X4),
-                scales=eps_scales[g, G][:],
-                in_=eps_bf[g, G][:].rearrange("p t m j -> p (t m j)"),
-            )
-
-        w_bf, w_codes, w_scales = {}, {}, {}
-
-        def inter(mat, g, h, engine):
-            dst = wt("w_bf", [P, 512, 4], BF16, 6)
-            w_bf[mat, g, h] = dst
-            src = (cu_raw if mat == "cu" else c_raw)[g][:, :, 512 * h : 512 * h + 512]
-            if engine == "s":
-                nc.scalar.copy(
-                    out=dst[:].rearrange("p (x i) j -> p x j i", i=4),
-                    in_=src.rearrange("p j (x i) -> p x j i", i=4),
-                )
-            elif engine == "v":
-                nc.vector.tensor_copy(
-                    out=dst[:].rearrange("p (x i) j -> p x j i", i=4),
-                    in_=src.rearrange("p j (x i) -> p x j i", i=4),
-                )
-            else:
-                for y in range(4):
-                    nc.gpsimd.tensor_scalar(
-                        out=dst[:, 128 * y : 128 * y + 128, :],
-                        in0=src.rearrange("p j z -> p z j")[:, 128 * y : 128 * y + 128, :],
-                        scalar1=1.0,
-                        scalar2=0.0,
-                        op0=MULT,
-                        op1=ADD,
-                    )
-
-        def quant_w(mat, g, h):
-            key = (mat, g, h)
-            w_codes[key] = kt("%s_codes%d%d" % key, [P, 512], U32)
-            w_scales[key] = kt("%s_scales%d%d" % key, [P, 512], U8)
-            nc.vector.quantize_mx(
-                out=w_codes[key][:].bitcast(FP8X4),
-                scales=w_scales[key][:],
-                in_=w_bf[key][:].rearrange("p z j -> p (z j)"),
-            )
-
-        k_ps, jac_bf, j_codes, j_scales = {}, {}, {}, {}
-
-        def stage1(k, ib, G):
-            b = bank("s1", [P, 4, P], F32, S1B)
-            cols = slice(P * ib, P * ib + P)
-            for t in range(4):
-                for g in range(2):
-                    nc.tensor.matmul_mx(
-                        out=b[:, t, :],
-                        lhsT=eps_codes[g, G][:, P * t : P * t + P].bitcast(FP8X4),
-                        lhsT_scale=eps_scales[g, G][:, P * t : P * t + P],
-                        rhs=n_codes[k][:, g, cols].bitcast(FP8X4),
-                        rhs_scale=n_scales[k][:, g, cols],
-                        start=(g == 0),
-                        stop=(g == 1),
-                    )
-            k_ps[k, ib, G] = b
-
-        def div_s(k, ib, G):
-            if k not in jac_bf:
-                jac_bf[k] = wt("jac_bf", [P, 2, ROWS, 4], BF16, 2)
-            b = k_ps.pop((k, ib, G))
+                nv[k] = rotating("nv", [P, 2, N], BF16, 2)
+            factors = v_row[:].rearrange("p (g x w e) -> p w g x e", g=2, w=2, e=2)[:, w]
             nc.vector.tensor_tensor(
-                out=jac_bf[k][:, G, P * ib : P * ib + P, :],
-                in0=b[:].rearrange("p t i -> p i t"),
-                in1=rs_row[:, ROWS * k + P * ib : ROWS * k + P * ib + P].unsqueeze(2).to_broadcast([P, P, 4]),
+                out=nv[k][:].rearrange("p b (g w x e) -> p w b g x e", g=2, w=2, e=2)[:, w],
+                in0=n_raw[k][:].rearrange("p b (g x w e) -> p w b g x e", g=2, w=2, e=2)[:, w],
+                in1=factors.unsqueeze(1).to_broadcast([P, 2, 2, P, 2]),
                 op=MULT,
             )
 
-        def quant_j(k):
-            j_codes[k] = wt("j_codes", [P, 2, ROWS], U32, 2)
-            j_scales[k] = wt("j_scales", [P, 2, ROWS], U8, 2)
-            nc.vector.quantize_mx(
-                out=j_codes[k][:].rearrange("p g i -> p (g i)").bitcast(FP8X4),
-                scales=j_scales[k][:].rearrange("p g i -> p (g i)"),
-                in_=jac_bf[k][:].rearrange("p g i t -> p (g i t)"),
+        def turn_n(k, g):
+            bank = turn_bank([P, 2, 2, P])
+            words = nv[k][:].bitcast(F32)
+            for w in range(2):
+                first = 256 * g + 128 * w
+                for b in range(2):
+                    nc.tensor.transpose(bank[:, w, b, :], words[:, b, first : first + P], identity[:])
+            turned["n_bf", k, g] = bank
+
+        def turn_l(k, g):
+            bank = turn_bank([P, 2, 2, P])
+            words = l_raw[k][:].bitcast(F32)
+            for w in range(2):
+                for b in range(2):
+                    nc.tensor.transpose(bank[:, w, b, :], words[:, b, 256 * g + w : 256 * g + 256 : 2], identity[:])
+            turned["l_bf", k, g] = bank
+
+        def lay_words(copy, out, bank):
+            copy(
+                out=out.rearrange("p i j -> p (i j)").bitcast(F32).rearrange("p (i w) -> p i w", w=2),
+                in_=bank[:].rearrange("p w b i -> p (b i) w"),
             )
 
-        o_ps, p_bf = {}, {}
+        def empty_turned(op, k, g):
+            if k not in op["values"]:
+                op["values"][k] = rotating(op["tag"], [P, 2, ROWS, 4], BF16, op["bufs"])
+            lay_words(by_scalar, op["values"][k][:, g], turned.pop((op["tag"], k, g)))
 
-        def stage2(k, h, ib, codes, scales, mat):
-            first = mat == "cu"
-            if first:
-                o_ps[k, h, ib] = bank("s2", [P, 512], F32, S2B)
-            cols = slice(P * ib, P * ib + P)
+        def quantize_rows(op, k):
+            op["codes"][k] = kept("%s_codes%d" % (op["tag"], k), [P, 2, ROWS], U32)
+            op["scales"][k] = kept("%s_scales%d" % (op["tag"], k), [P, 2, ROWS], U8)
+            quantize(
+                op["codes"][k][:].rearrange("p g i -> p (g i)"),
+                op["scales"][k][:].rearrange("p g i -> p (g i)"),
+                op["values"][k][:].rearrange("p g i j -> p (g i j)"),
+            )
+
+        eps, eps_codes, eps_scales = {}, {}, {}
+
+        def scale_a(g, G, t):
+            if (g, G) not in eps:
+                eps[g, G] = rotating("eps", [P, 4, P, 4], BF16, 3)
+            species = slice(PASS * G, PASS * G + PASS)
+            e_row = e_banks[G][:, t].rearrange("p (y i) -> p y i", i=4)
+            nc.vector.tensor_tensor(
+                out=eps[g, G][:, t].rearrange("p (y i) j -> p y j i", i=4),
+                in0=a_raw[g][:, :, species].rearrange("p j (y t i) -> p t y j i", t=4, i=4)[:, t],
+                in1=e_row.unsqueeze(2).to_broadcast([P, P // 4, 4, 4]),
+                op=MULT,
+            )
+
+        def quantize_eps(g, G):
+            eps_codes[g, G] = kept("eps_codes%d%d" % (g, G), [P, 4 * P], U32)
+            eps_scales[g, G] = kept("eps_scales%d%d" % (g, G), [P, 4 * P], U8)
+            quantize(eps_codes[g, G][:], eps_scales[g, G][:], eps[g, G][:].rearrange("p t m j -> p (t m j)"))
+
+        c_op = {"tag": "c", "raw": c_raw, "values": {}, "codes": {}, "scales": {}}
+        cu_op = {"tag": "cu", "raw": cu_raw, "values": {}, "codes": {}, "scales": {}}
+
+        def interleave(op, g, h, copy):
+            op["values"][g, h] = rotating("w_bf", [P, PASS, 4], BF16, 6)
+            copy(
+                out=op["values"][g, h][:].rearrange("p (x i) j -> p x j i", i=4),
+                in_=op["raw"][g][:, :, halves[h]].rearrange("p j (x i) -> p x j i", i=4),
+            )
+
+        def quantize_columns(op, g, h):
+            op["codes"][g, h] = kept("%s_codes%d%d" % (op["tag"], g, h), [P, PASS], U32)
+            op["scales"][g, h] = kept("%s_scales%d%d" % (op["tag"], g, h), [P, PASS], U8)
+            quantize(op["codes"][g, h][:], op["scales"][g, h][:], op["values"][g, h][:].rearrange("p z j -> p (z j)"))
+
+        k_banks, jac, jac_codes, jac_scales = {}, {}, {}, {}
+
+        def multiply_nv_eps(k, b, G):
+            bank = k_bank()
+            rows = slice(P * b, P * b + P)
+            for t in range(4):
+                cols = slice(P * t, P * t + P)
+                for g in range(2):
+                    multiply(
+                        bank[:, t, :],
+                        (eps_codes[g, G][:, cols], eps_scales[g, G][:, cols]),
+                        (n_op["codes"][k][:, g, rows], n_op["scales"][k][:, g, rows]),
+                        start=(g == 0),
+                        stop=(g == 1),
+                    )
+            k_banks[k, b, G] = bank
+
+        def divide_by_s(k, b, G):
+            if k not in jac:
+                jac[k] = rotating("jac", [P, 2, ROWS, 4], BF16, 2)
+            row0 = ROWS * k + P * b
+            nc.vector.tensor_tensor(
+                out=jac[k][:, G, P * b : P * b + P, :],
+                in0=k_banks.pop((k, b, G))[:].rearrange("p t i -> p i t"),
+                in1=inv_s_row[:, row0 : row0 + P].unsqueeze(2).to_broadcast([P, P, 4]),
+                op=MULT,
+            )
+
+        def quantize_jac(k):
+            jac_codes[k] = rotating("jac_codes", [P, 2, ROWS], U32, 2)
+            jac_scales[k] = rotating("jac_scales", [P, 2, ROWS], U8, 2)
+            quantize(
+                jac_codes[k][:].rearrange("p G i -> p (G i)"),
+                jac_scales[k][:].rearrange("p G i -> p (G i)"),
+                jac[k][:].rearrange("p G i t -> p (G i t)"),
+            )
+
+        row_banks, rounded = {}, {}
+
+        def start_rows(k, h, b):
+            row_banks[k, h, b] = row_bank([P, PASS])
+            rows = slice(P * b, P * b + P)
             for g in range(2):
-                nc.tensor.matmul_mx(
-                    out=o_ps[k, h, ib][:],
-                    lhsT=codes[:, g, cols].bitcast(FP8X4),
-                    lhsT_scale=scales[:, g, cols],
-                    rhs=w_codes[mat, g, h][:].bitcast(FP8X4),
-                    rhs_scale=w_scales[mat, g, h][:],
-                    start=(first and g == 0),
-                    stop=(not first and g == 1),
+                multiply(
+                    row_banks[k, h, b][:],
+                    (l_op["codes"][k][:, g, rows], l_op["scales"][k][:, g, rows]),
+                    (cu_op["codes"][g, h][:], cu_op["scales"][g, h][:]),
+                    start=(g == 0),
+                    stop=False,
                 )
 
-        def stage2_l(k, h, ib):
-            stage2(k, h, ib, l_codes[k], l_scales[k], "cu")
+        def finish_rows(k, h, b):
+            rows = slice(P * b, P * b + P)
+            for G in range(2):
+                multiply(
+                    row_banks[k, h, b][:],
+                    (jac_codes[k][:, G, rows], jac_scales[k][:, G, rows]),
+                    (c_op["codes"][G, h][:], c_op["scales"][G, h][:]),
+                    start=False,
+                    stop=(G == 1),
+                )
 
-        def stage2_j(k, h, ib):
-            stage2(k, h, ib, j_codes[k], j_scales[k], "c")
+        def empty_rows(k, h, b, round_with, bank_first):
+            bank = row_banks.pop((k, h, b))
+            small = rotating("rounded", [P, PASS], BF16, 6)
+            rows = rotating("rows", [P, PASS], F32, 4)
+            if not bank_first:
+                nc.scalar.copy(out=rows[:], in_=bank[:])
+            round_with(
+                out=small[:].rearrange("p (w x e) -> p w x e", w=2, e=2),
+                in_=(bank if bank_first else rows)[:].rearrange("p (x w e) -> p w x e", w=2, e=2),
+            )
+            if bank_first:
+                nc.scalar.copy(out=rows[:], in_=bank[:])
+            rounded[k, h, b] = small
+            row0 = ROWS * k + P * b
+            nc.sync.dma_start(out=out_0[row0 : row0 + P, halves[h]], in_=rows[:])
 
-        def out_rows(k, h, ib, copy, round_v=False):
-            b = o_ps.pop((k, h, ib))
-            p_bf[k, h, ib] = wt("p_bf", [P, 512], BF16, 6)
-            o_f = wt("o_f", [P, 512], F32, 4)
-
-            def turned(t):
-                return t[:].rearrange("p (m u e) -> p u m e", u=2, e=2)
-
-            to = p_bf[k, h, ib][:].rearrange("p (u m e) -> p u m e", u=2, e=2)
-            if round_v:
-                copy(out=o_f[:], in_=b[:])
-                nc.vector.tensor_copy(out=to, in_=turned(o_f))
-            else:
-                copy(out=to, in_=turned(b))
-                copy(out=o_f[:], in_=b[:])
-            i0 = ROWS * k + P * ib
-            nc.sync.dma_start(out=out_0[i0 : i0 + P, 512 * h : 512 * h + 512], in_=o_f[:])
-
-        pt_bf = {}
-        p_scales = kt("p_scales", [P, 2, D], U8)
-        words_out = out_1.rearrange("g p m t -> g p (m t)").bitcast(I32)
+        both = [0, 1]
+        p_values = {}
+        p_scales = kept("p_scales", [P, 2, N], U8)
+        words_out = out_1.rearrange("g p i j -> g p (i j)").bitcast(I32)
         scales_out = out_2.bitcast(I32)
 
-        def turn_p(k, h):
-            b = bank("tr", [P, 2, 2, P], F32, TRB)
-            for ib in range(2):
-                words = p_bf.pop((k, h, ib))[:].bitcast(F32)
-                for u in range(2):
-                    nc.tensor.transpose(b[:, u, ib, :], words[:, P * u : P * u + P], ident[:])
-            tr_ps["p", k, h] = b
+        def turn_p(k, h, blocks):
+            bank = turn_bank([P, 2, len(blocks), P])
+            for x, b in enumerate(blocks):
+                words = rounded.pop((k, h, b))[:].bitcast(F32)
+                for w in range(2):
+                    nc.tensor.transpose(bank[:, w, x, :], words[:, P * w : P * w + P], identity[:])
+            turned["p", k, h, blocks[0]] = bank
 
-        def out_p(k, h, copy):
-            b = tr_ps.pop(("p", k, h))
-            pt_bf[k, h] = wt("pt_bf", [P, ROWS, 4], BF16, 3)
-            copy(
-                out=pt_bf[k, h][:].rearrange("p i t -> p (i t)").bitcast(F32).rearrange("p (i u) -> p i u", u=2),
-                in_=b[:].rearrange("p u b i -> p (b i) u"),
-            )
+        def empty_p(k, h, blocks, copy):
+            values = rotating("p_values", [P, P * len(blocks), 4], BF16, 3)
+            lay_words(copy, values[:], turned.pop(("p", k, h, blocks[0])))
+            p_values[k, h, blocks[0]] = values
 
-        def quant_p(k, h):
-            pw = wt("pw", [P, ROWS], U32, 3)
-            nc.vector.quantize_mx(
-                out=pw[:].bitcast(FP8X4),
-                scales=p_scales[:, h, ROWS * k : ROWS * k + ROWS],
-                in_=pt_bf.pop((k, h))[:].rearrange("p i t -> p (i t)"),
-            )
-            nc.sync.dma_start(out=words_out[h, :, ROWS * k : ROWS * k + ROWS], in_=pw[:].bitcast(I32))
+        def quantize_p(k, h, blocks):
+            row0 = ROWS * k + P * blocks[0]
+            rows = slice(row0, row0 + P * len(blocks))
+            codes = rotating("p_codes", [P, P * len(blocks)], U32, 3)
+            quantize(codes[:], p_scales[:, h, rows], p_values.pop((k, h, blocks[0]))[:].rearrange("p i j -> p (i j)"))
+            nc.sync.dma_start(out=words_out[h, :, rows], in_=codes[:].bitcast(I32))
 
-        def store_scales(i0, i1):
+        def store_scales(row0, row1):
+            quads = slice(row0 // 4, row1 // 4)
             for Q in range(4):
                 nc.sync.dma_start(
-                    out=scales_out[:, 4 * Q : 4 * Q + 4, i0 // 4 : i1 // 4].rearrange("g r i -> r g i"),
-                    in_=p_scales[32 * Q : 32 * Q + 4, :, :].bitcast(I32)[:, :, i0 // 4 : i1 // 4],
+                    out=scales_out[:, 4 * Q : 4 * Q + 4, quads].rearrange("g r i -> r g i"),
+                    in_=p_scales[32 * Q : 32 * Q + 4, :, :].bitcast(I32)[:, :, quads],
                 )
 
-        S_COPY, V_COPY = nc.scalar.copy, nc.vector.tensor_copy
-        T4 = range(4)
-        spread_e(0)
-        load_a(1)
-        mul_e(1, 0, 0)
-        load_a(0)
-        load_cu(1)
-        spread_e(1)
-        mul_e(1, 0, 2)
-        spread_v()
-        load_l(0)
-        mul_e(1, 1, 0)
-        inter("cu", 1, 1, "s")
-        mul_e(1, 0, 3)
-        mul_e(1, 1, 1)
-        load_n(0)
-        mul_e(1, 1, 2)
-        mul_e(1, 0, 1)
-        mul_e(0, 0, 0)
-        quant_e(1, 0)
-        load_n(1)
-        spread_rs(0)
-        load_l(1)
-        mul_e(0, 0, 3)
-        mul_e(0, 1, 2)
-        mul_e(0, 0, 1)
-        load_n(3)
-        mul_n(0, 0, nc.vector)
-        turn_l(0, 1)
-        mul_n(0, 1, nc.vector)
-        out_l(0, 1, S_COPY)
-        turn_l(0, 0)
-        mul_n(1, 1, nc.vector)
-        out_l(0, 0, S_COPY)
-        spread_rs(1)
-        load_l(2)
-        mul_n(1, 0, nc.vector)
-        mul_e(0, 1, 3)
-        mul_e(0, 0, 2)
-        turn_n(0, 0)
-        out_n(0, 0, S_COPY)
-        load_cu(0)
-        turn_n(0, 1)
-        turn_n(1, 1)
-        out_n(0, 1, S_COPY)
-        inter("cu", 1, 0, "s")
-        out_n(1, 1, S_COPY)
-        quant_l(0)
-        quant_e(0, 0)
-        turn_n(1, 0)
-        quant_n(0)
-        load_n(2)
-        mul_n(3, 1, nc.vector)
-        out_n(1, 0, S_COPY)
-        mul_e(1, 1, 3)
-        turn_l(1, 0)
-        mul_e(0, 1, 1)
-        mul_e(0, 1, 0)
-        mul_n(3, 0, nc.vector)
-        quant_e(0, 1)
-        inter("cu", 0, 0, "s")
-        stage1(0, 1, 0)
-        load_c(1)
-        out_l(1, 0, S_COPY)
-        quant_e(1, 1)
-        turn_l(1, 1)
-        stage1(0, 0, 0)
-        div_s(0, 1, 0)
-        div_s(0, 0, 0)
-        quant_n(1)
-        stage1(0, 0, 1)
+        load_grouped(a_raw, a, 1, whole)
+        load_grouped(cu_raw, cu, 1, whole)
+        load_grouped(a_raw, a, 0, halves[0])
+        load_rows(l_raw, l, 0)
+        load_grouped(a_raw, a, 0, halves[1])
+        load_rows(n_raw, n, 0)
+        load_rows(l_raw, l, 1)
+        load_rows(n_raw, n, 1)
+        load_rows(l_raw, l, 3)
+        load_grouped(cu_raw, cu, 0, halves[0])
+        load_rows(n_raw, n, 2)
         load_c(0)
-        stage1(0, 1, 1)
-        turn_n(3, 1)
-        quant_w("cu", 0, 0)
-        out_l(1, 1, S_COPY)
-        inter("c", 1, 0, "s")
-        quant_w("cu", 1, 0)
-        turn_l(2, 1)
-        stage2_l(0, 0, 1)
-        out_n(3, 1, S_COPY)
-        div_s(0, 0, 1)
-        div_s(0, 1, 1)
-        mul_n(2, 0, nc.vector)
-        out_l(2, 1, S_COPY)
-        stage2_l(0, 0, 0)
-        stage1(1, 0, 0)
-        stage1(1, 1, 0)
-        mul_n(2, 1, nc.vector)
-        quant_l(1)
-        load_l(3)
-        div_s(1, 0, 0)
-        turn_n(2, 0)
-        div_s(1, 1, 0)
-        quant_w("c", 1, 0)
-        turn_n(2, 1)
-        inter("c", 0, 0, "s")
-        stage2_l(1, 0, 0)
-        quant_w("c", 0, 0)
-        stage2_l(1, 0, 1)
-        quant_j(0)
-        stage1(1, 0, 1)
-        stage1(1, 1, 1)
-        out_n(2, 0, S_COPY)
-        out_n(2, 1, S_COPY)
-        inter("c", 1, 1, "s")
-        turn_n(3, 0)
-        div_s(1, 0, 1)
+
+        interleave(cu_op, 1, 0, by_scalar)
+        spread_e(0)
+        scale_a(1, 0, 3)
+        spread_e(1)
+        interleave(cu_op, 1, 1, by_scalar)
+        scale_a(1, 0, 0)
+        spread_v()
+        turn_l(0, 0)
+        scale_a(1, 1, 0)
+        scale_a(1, 0, 2)
+        turn_l(0, 1)
+        scale_a(1, 1, 2)
+        scale_a(1, 0, 1)
+        spread_inv_s(0)
+        scale_a(0, 0, 1)
+        empty_turned(l_op, 0, 0)
+        scale_a(1, 1, 1)
+        empty_turned(l_op, 0, 1)
+        quantize_eps(1, 0)
+        scale_a(0, 0, 2)
+        scale_a(0, 1, 1)
+        scale_a(0, 0, 0)
+        scale_n(0, 1)
+        spread_inv_s(1)
+        scale_n(0, 0)
+        scale_a(0, 0, 3)
+        scale_a(1, 1, 3)
+        scale_n(1, 1)
+        turn_l(1, 1)
+        scale_n(1, 0)
+        empty_turned(l_op, 1, 1)
+        turn_n(0, 0)
+        scale_a(0, 1, 0)
+        turn_n(0, 1)
         turn_l(3, 0)
-        stage2_j(0, 0, 0)
-        quant_n(2)
-        stage2_j(0, 0, 1)
-        div_s(1, 1, 1)
-        quant_j(1)
-        stage1(2, 0, 1)
-        quant_w("cu", 1, 1)
-        stage1(2, 1, 0)
-        stage2_j(1, 0, 0)
-        div_s(2, 0, 1)
-        inter("cu", 0, 1, "v")
-        div_s(2, 1, 0)
-        out_l(3, 0, S_COPY)
-        quant_w("cu", 0, 1)
-        quant_w("c", 1, 1)
-        out_n(3, 0, S_COPY)
-        out_rows(0, 0, 1, S_COPY, True)
-        inter("c", 0, 1, "s")
-        out_rows(0, 0, 0, S_COPY)
-        out_rows(1, 0, 0, S_COPY)
-        quant_w("c", 0, 1)
-        stage2_j(1, 0, 1)
+        quantize_eps(0, 0)
+        empty_turned(n_op, 0, 0)
+        scale_a(0, 1, 2)
+        turn_n(1, 0)
+        empty_turned(n_op, 0, 1)
+        load_rows(l_raw, l, 2)
+        turn_n(1, 1)
+        quantize_rows(n_op, 0)
+        interleave(cu_op, 0, 0, by_scalar)
+        scale_a(0, 1, 3)
+        scale_n(2, 1)
+        load_c(1)
+
+        multiply_nv_eps(0, 0, 0)
+        scale_n(2, 0)
+        quantize_eps(1, 1)
+        empty_turned(l_op, 3, 0)
+        divide_by_s(0, 0, 0)
+        empty_turned(n_op, 1, 1)
+        multiply_nv_eps(0, 1, 0)
+        quantize_eps(0, 1)
+        divide_by_s(0, 1, 0)
+        empty_turned(n_op, 1, 0)
+        turn_n(2, 0)
+        turn_n(2, 1)
+        load_grouped(cu_raw, cu, 0, halves[1])
+        turn_l(1, 0)
+        interleave(c_op, 0, 0, by_scalar)
+        quantize_rows(n_op, 1)
+        multiply_nv_eps(0, 0, 1)
+        multiply_nv_eps(0, 1, 1)
+        empty_turned(n_op, 2, 0)
         turn_l(2, 0)
+        load_rows(n_raw, n, 3)
+        empty_turned(n_op, 2, 1)
+        turn_l(2, 1)
+        quantize_columns(cu_op, 0, 0)
+        empty_turned(l_op, 1, 0)
+        divide_by_s(0, 0, 1)
+        interleave(c_op, 1, 0, by_scalar)
+        divide_by_s(0, 1, 1)
+        quantize_rows(l_op, 0)
+        quantize_columns(cu_op, 1, 0)
+        multiply_nv_eps(1, 0, 1)
         turn_l(3, 1)
-        stage1(2, 1, 1)
-        out_l(2, 0, V_COPY)
-        stage1(2, 0, 0)
-        stage2_l(1, 1, 1)
-        quant_n(3)
-        stage2_l(0, 1, 1)
-        stage2_l(0, 1, 0)
-        out_rows(1, 0, 1, S_COPY, True)
-        div_s(2, 1, 1)
-        stage2_j(1, 1, 1)
-        quant_l(2)
-        stage2_l(1, 1, 0)
-        stage2_j(0, 1, 1)
-        div_s(2, 0, 0)
-        stage2_j(0, 1, 0)
-        stage1(3, 1, 0)
-        out_l(3, 1, S_COPY)
-        turn_p(1, 0)
-        turn_p(0, 0)
-        out_rows(1, 1, 1, S_COPY)
-        out_rows(0, 1, 1, V_COPY)
-        stage2_l(2, 0, 0)
-        quant_j(2)
-        out_rows(0, 1, 0, S_COPY, True)
-        stage1(3, 0, 1)
-        out_p(1, 0, S_COPY)
-        out_p(0, 0, S_COPY)
-        quant_p(0, 0)
-        stage2_j(1, 1, 0)
-        div_s(3, 1, 0)
-        stage2_j(2, 0, 0)
-        stage2_l(2, 0, 1)
-        stage2_j(2, 0, 1)
-        div_s(3, 0, 1)
-        stage1(3, 0, 0)
-        out_rows(2, 0, 0, S_COPY, True)
-        stage2_l(2, 1, 1)
-        out_rows(1, 1, 0, S_COPY)
-        stage1(3, 1, 1)
-        turn_p(1, 1)
-        quant_l(3)
-        turn_p(0, 1)
-        div_s(3, 0, 0)
-        div_s(3, 1, 1)
-        quant_p(1, 0)
-        quant_j(3)
-        out_rows(2, 0, 1, S_COPY)
-        stage2_l(2, 1, 0)
-        stage2_j(2, 1, 1)
-        stage2_l(3, 0, 0)
-        out_p(1, 1, S_COPY)
-        stage2_l(3, 1, 0)
-        stage2_j(2, 1, 0)
-        out_p(0, 1, S_COPY)
-        out_rows(2, 1, 1, S_COPY)
-        quant_p(1, 1)
-        out_rows(2, 1, 0, S_COPY, True)
-        stage2_j(3, 1, 0)
-        stage2_j(3, 0, 0)
-        quant_p(0, 1)
-        turn_p(2, 1)
-        turn_p(2, 0)
-        out_rows(3, 1, 0, S_COPY, True)
-        out_p(2, 0, V_COPY)
-        stage2_l(3, 0, 1)
-        out_p(2, 1, S_COPY)
-        quant_p(2, 1)
-        out_rows(3, 0, 0, S_COPY, True)
-        quant_p(2, 0)
-        stage2_j(3, 0, 1)
-        store_scales(0, ROWS * 3)
-        stage2_l(3, 1, 1)
-        stage2_j(3, 1, 1)
-        out_rows(3, 0, 1, S_COPY, True)
-        out_rows(3, 1, 1, S_COPY)
-        turn_p(3, 0)
-        turn_p(3, 1)
-        out_p(3, 0, V_COPY)
-        quant_p(3, 0)
-        out_p(3, 1, S_COPY)
-        quant_p(3, 1)
-        store_scales(ROWS * 3, D)
+        quantize_jac(0)
+        multiply_nv_eps(1, 1, 0)
+        divide_by_s(1, 0, 1)
+
+        start_rows(0, 0, 1)
+        quantize_columns(c_op, 0, 0)
+        quantize_columns(c_op, 1, 0)
+        multiply_nv_eps(1, 1, 1)
+        start_rows(0, 0, 0)
+        divide_by_s(1, 1, 0)
+        finish_rows(0, 0, 0)
+        multiply_nv_eps(1, 0, 0)
+        quantize_rows(n_op, 2)
+        divide_by_s(1, 1, 1)
+        interleave(c_op, 0, 1, by_scalar)
+        finish_rows(0, 0, 1)
+        quantize_rows(l_op, 1)
+        multiply_nv_eps(2, 0, 0)
+        divide_by_s(1, 0, 0)
+        start_rows(1, 0, 1)
+        divide_by_s(2, 0, 0)
+        quantize_jac(1)
+        quantize_columns(cu_op, 1, 1)
+        scale_n(3, 0)
+        scale_n(3, 1)
+        interleave(cu_op, 0, 1, by_scalar)
+        quantize_columns(cu_op, 0, 1)
+        interleave(c_op, 1, 1, by_vector)
+        multiply_nv_eps(2, 0, 1)
+        quantize_columns(c_op, 0, 1)
+        multiply_nv_eps(2, 1, 0)
+        quantize_columns(c_op, 1, 1)
+        finish_rows(1, 0, 1)
+        empty_rows(0, 0, 1, by_vector, False)
+        divide_by_s(2, 0, 1)
+        empty_turned(l_op, 2, 0)
+        start_rows(1, 0, 0)
+        empty_turned(l_op, 2, 1)
+        finish_rows(1, 0, 0)
+        empty_rows(0, 0, 0, by_vector, False)
+        turn_n(3, 1)
+        turn_n(3, 0)
+        empty_rows(1, 0, 1, by_vector, False)
+
+        start_rows(0, 1, 0)
+        start_rows(1, 1, 0)
+        empty_rows(1, 0, 0, by_vector, False)
+        empty_turned(l_op, 3, 1)
+        start_rows(1, 1, 1)
+        finish_rows(0, 1, 0)
+        finish_rows(1, 1, 0)
+        finish_rows(1, 1, 1)
+        empty_turned(n_op, 3, 0)
+        multiply_nv_eps(2, 1, 1)
+        empty_turned(n_op, 3, 1)
+        divide_by_s(2, 1, 0)
+        quantize_rows(n_op, 3)
+        turn_p(0, 0, both)
+        empty_rows(0, 1, 0, by_scalar, True)
+        turn_p(1, 0, both)
+        start_rows(0, 1, 1)
+        finish_rows(0, 1, 1)
+        divide_by_s(2, 1, 1)
+        quantize_rows(l_op, 2)
+        multiply_nv_eps(3, 0, 0)
+        empty_rows(1, 1, 1, by_vector, False)
+        empty_p(0, 0, both, by_scalar)
+        empty_rows(1, 1, 0, by_scalar, True)
+        empty_rows(0, 1, 1, by_scalar, True)
+        quantize_jac(2)
+        multiply_nv_eps(3, 1, 1)
+        start_rows(2, 1, 0)
+        divide_by_s(3, 0, 0)
+        divide_by_s(3, 1, 1)
+        finish_rows(2, 1, 0)
+        empty_p(1, 0, both, by_scalar)
+        start_rows(2, 1, 1)
+        quantize_p(0, 0, both)
+        finish_rows(2, 1, 1)
+        empty_rows(2, 1, 0, by_vector, True)
+        multiply_nv_eps(3, 1, 0)
+        quantize_rows(l_op, 3)
+        multiply_nv_eps(3, 0, 1)
+        divide_by_s(3, 1, 0)
+        turn_p(0, 1, both)
+        turn_p(1, 1, both)
+        empty_rows(2, 1, 1, by_scalar, True)
+        divide_by_s(3, 0, 1)
+        turn_p(2, 1, both)
+        quantize_p(1, 0, both)
+
+        start_rows(2, 0, 0)
+        empty_p(0, 1, both, by_scalar)
+        finish_rows(2, 0, 0)
+        start_rows(2, 0, 1)
+        empty_p(2, 1, both, by_vector)
+        finish_rows(2, 0, 1)
+        start_rows(3, 0, 0)
+        empty_p(1, 1, both, by_scalar)
+        quantize_jac(3)
+        quantize_p(2, 1, both)
+        finish_rows(3, 0, 0)
+        quantize_p(0, 1, both)
+        empty_rows(2, 0, 0, by_vector, False)
+        start_rows(3, 1, 0)
+        finish_rows(3, 1, 0)
+        empty_rows(2, 0, 1, by_vector, True)
+        quantize_p(1, 1, both)
+        turn_p(2, 0, both)
+        empty_rows(3, 0, 0, by_vector, True)
+        turn_p(3, 0, [0])
+        start_rows(3, 0, 1)
+        empty_rows(3, 1, 0, by_vector, True)
+        empty_p(3, 0, [0], by_scalar)
+        finish_rows(3, 0, 1)
+        empty_p(2, 0, both, by_vector)
+        start_rows(3, 1, 1)
+        quantize_p(3, 0, [0])
+        quantize_p(2, 0, both)
+        store_scales(0, 3 * ROWS)
+        finish_rows(3, 1, 1)
+        empty_rows(3, 0, 1, by_vector, True)
+        turn_p(3, 1, [0])
+        turn_p(3, 0, [1])
+        empty_rows(3, 1, 1, by_vector, True)
+        empty_p(3, 1, [0], by_scalar)
+        turn_p(3, 1, [1])
+        empty_p(3, 0, [1], by_vector)
+        quantize_p(3, 1, [0])
+        quantize_p(3, 0, [1])
+        empty_p(3, 1, [1], by_scalar)
+        quantize_p(3, 1, [1])
+        store_scales(3 * ROWS, N)

from contextlib import ExitStack

import concourse.mybir as mybir
from concourse.masks import make_identity

N = 1024
FLOPS = 3 * 2 * N * N * N

F32 = mybir.dt.float32
BF16 = mybir.dt.bfloat16
U32 = mybir.dt.uint32
I32 = mybir.dt.int32
U8 = mybir.dt.uint8
FP8X4 = mybir.dt.float8_e4m3fn_x4
MULT = mybir.AluOpType.mult
ADD = mybir.AluOpType.add

P = 128
PASS = 512
ROWS = 256
SUPERBLOCKS = N // ROWS

TURN_BANKS = 3
K_BANKS = 2
ROW_BANKS = 3


def tile_relativefluctuationcovariancedrift_kernel(tc, n, v, a, s, c, l, cu, out_0, out_1, out_2):
    nc = tc.nc
    by_vector = nc.vector.tensor_copy
    by_scalar = nc.scalar.copy

    with ExitStack() as ctx:
        keep = ctx.enter_context(tc.tile_pool(name="keep", bufs=1))
        work = ctx.enter_context(tc.tile_pool(name="work", bufs=1))
        psum = ctx.enter_context(tc.psum_pool(name="psum", bufs=1))
        ctx.enter_context(tc.manual_schedule())

        def kept(name, shape, dtype):
            return keep.tile(shape, dtype, name=name, tag=name, align_bytes=64)

        def rotating(tag, shape, dtype, bufs):
            return work.tile(shape, dtype, name=tag, tag=tag, bufs=bufs, align_bytes=64)

        def turn_bank(shape, dtype=F32):
            return psum.tile(shape, dtype, name="turn_bank", tag="turn_bank", bufs=TURN_BANKS)

        def k_bank():
            return psum.tile([P, 4, P], F32, name="k_bank", tag="k_bank", bufs=K_BANKS)

        def row_bank(shape):
            return psum.tile(shape, F32, name="row_bank", tag="row_bank", bufs=ROW_BANKS)

        def quantize(codes, scales, values):
            nc.vector.quantize_mx(out=codes.bitcast(FP8X4), scales=scales, in_=values)

        def multiply(out, stationary, moving, start, stop):
            nc.tensor.matmul_mx(
                out=out,
                lhsT=stationary[0].bitcast(FP8X4),
                lhsT_scale=stationary[1],
                rhs=moving[0].bitcast(FP8X4),
                rhs_scale=moving[1],
                start=start,
                stop=stop,
            )

        vector_rows = kept("vector_rows", [P, P], BF16)
        nc.vector.memset(vector_rows[:], 0.0)
        identity = kept("identity", [P, P], F32)
        make_identity(nc, identity[:])
        identity_bf16 = kept("identity_bf16", [P, P], BF16)
        nc.vector.tensor_copy(out=identity_bf16[:], in_=identity[:])

        for G in range(2):
            nc.sync.dma_start(
                out=vector_rows[4 * G : 4 * G + 4, :].rearrange("t (y i) -> t y i", i=4),
                in_=s[PASS * G : PASS * G + PASS].rearrange("(y t i) -> t y i", t=4, i=4),
            )
        nc.sync.dma_start(out=vector_rows[8:16, :], in_=s.rearrange("(x p) -> x p", p=P))
        nc.sync.dma_start(out=vector_rows[16:24, :], in_=v.rearrange("(x p) -> x p", p=P))

        columns = turn_bank([P, P], BF16)
        nc.tensor.transpose(columns[:], vector_rows[:], identity_bf16[:])
        s_cols = kept("s_cols", [P, 16], F32)
        nc.vector.tensor_copy(out=s_cols[:], in_=columns[:, 0:16])
        s_squared = kept("s_squared", [P, 8], F32)
        nc.vector.tensor_tensor(out=s_squared[:], in0=s_cols[:, 0:8], in1=s_cols[:, 0:8], op=MULT)
        half_sum = kept("half_sum", [P, 8], F32)
        nc.vector.tensor_scalar(out=half_sum[:], in0=s_squared[:], scalar1=0.5, scalar2=0.5, op0=MULT, op1=ADD)
        e_cols = kept("e_cols", [P, 8], F32)
        nc.vector.reciprocal(out=e_cols[:], in_=half_sum[:])
        inv_s_cols = kept("inv_s_cols", [P, 8], F32)
        nc.vector.reciprocal(out=inv_s_cols[:], in_=s_cols[:, 8:16])
        v_cols = kept("v_cols", [P, 8], BF16)
        nc.vector.tensor_copy(out=v_cols[:], in_=columns[:, 16:24])

        v_row = kept("v_row", [P, N], BF16)
        inv_s_row = kept("inv_s_row", [P, N], F32)
        e_banks = {}

        def spread_v():
            b = turn_bank([P, 8, P], BF16)
            for x in range(8):
                nc.tensor.transpose(b[:, x, :], v_cols[:, x : x + 1].to_broadcast([P, P]), identity_bf16[:])
            nc.scalar.copy(out=v_row[:], in_=b[:].rearrange("p x r -> p (x r)"))

        def spread_inv_s(half):
            b = k_bank()
            for x in range(4):
                col = 4 * half + x
                nc.tensor.transpose(b[:, x, :], inv_s_cols[:, col : col + 1].to_broadcast([P, P]), identity[:])
            nc.scalar.copy(out=inv_s_row[:, PASS * half : PASS * half + PASS], in_=b[:].rearrange("p x i -> p (x i)"))

        def spread_e(G):
            e_banks[G] = row_bank([P, 4, P])
            for t in range(4):
                col = 4 * G + t
                nc.tensor.transpose(e_banks[G][:, t, :], e_cols[:, col : col + 1].to_broadcast([P, P]), identity[:])

        a_raw = [kept("a_raw%d" % g, [P, 4, N], BF16) for g in range(2)]
        cu_raw = [kept("cu_raw%d" % g, [P, 4, N], BF16) for g in range(2)]
        c_raw = [kept("c_raw%d" % G, [P, 4, N], BF16) for G in range(2)]
        n_raw, l_raw = {}, {}
        whole = slice(0, N)
        halves = [slice(0, PASS), slice(PASS, N)]

        def load_grouped(raw, source, g, cols):
            rows = source[PASS * g : PASS * g + PASS, cols]
            nc.sync.dma_start(out=raw[g][:, :, cols], in_=rows.rearrange("(p j) w -> p j w", j=4))

        def load_c(G):
            rows = c[PASS * G : PASS * G + PASS, :].rearrange("(y t i) z -> t y i z", t=4, i=4)
            for t in range(4):
                nc.sync.dma_start(out=c_raw[G][:, t, :], in_=rows[t])

        def load_rows(raw, source, k):
            tag = "n_raw" if raw is n_raw else "l_raw"
            raw[k] = rotating(tag, [P, 2, N], BF16, 3)
            rows = source[ROWS * k : ROWS * k + ROWS, :]
            nc.sync.dma_start(out=raw[k][:], in_=rows.rearrange("(b p) r -> p b r", p=P))

        nv, turned = {}, {}
        n_op = {"tag": "n_bf", "bufs": 2, "values": {}, "codes": {}, "scales": {}}
        l_op = {"tag": "l_bf", "bufs": 3, "values": {}, "codes": {}, "scales": {}}

        def scale_n(k, w):
            if k not in nv:
                nv[k] = rotating("nv", [P, 2, N], BF16, 2)
            factors = v_row[:].rearrange("p (g x w e) -> p w g x e", g=2, w=2, e=2)[:, w]
            nc.vector.tensor_tensor(
                out=nv[k][:].rearrange("p b (g w x e) -> p w b g x e", g=2, w=2, e=2)[:, w],
                in0=n_raw[k][:].rearrange("p b (g x w e) -> p w b g x e", g=2, w=2, e=2)[:, w],
                in1=factors.unsqueeze(1).to_broadcast([P, 2, 2, P, 2]),
                op=MULT,
            )

        def turn_n(k, g):
            bank = turn_bank([P, 2, 2, P])
            words = nv[k][:].bitcast(F32)
            for w in range(2):
                first = 256 * g + 128 * w
                for b in range(2):
                    nc.tensor.transpose(bank[:, w, b, :], words[:, b, first : first + P], identity[:])
            turned["n_bf", k, g] = bank

        def turn_l(k, g):
            bank = turn_bank([P, 2, 2, P])
            words = l_raw[k][:].bitcast(F32)
            for w in range(2):
                for b in range(2):
                    nc.tensor.transpose(bank[:, w, b, :], words[:, b, 256 * g + w : 256 * g + 256 : 2], identity[:])
            turned["l_bf", k, g] = bank

        def lay_words(copy, out, bank):
            copy(
                out=out.rearrange("p i j -> p (i j)").bitcast(F32).rearrange("p (i w) -> p i w", w=2),
                in_=bank[:].rearrange("p w b i -> p (b i) w"),
            )

        def empty_turned(op, k, g):
            if k not in op["values"]:
                op["values"][k] = rotating(op["tag"], [P, 2, ROWS, 4], BF16, op["bufs"])
            lay_words(by_scalar, op["values"][k][:, g], turned.pop((op["tag"], k, g)))

        def quantize_rows(op, k):
            op["codes"][k] = kept("%s_codes%d" % (op["tag"], k), [P, 2, ROWS], U32)
            op["scales"][k] = kept("%s_scales%d" % (op["tag"], k), [P, 2, ROWS], U8)
            quantize(
                op["codes"][k][:].rearrange("p g i -> p (g i)"),
                op["scales"][k][:].rearrange("p g i -> p (g i)"),
                op["values"][k][:].rearrange("p g i j -> p (g i j)"),
            )

        eps, eps_codes, eps_scales = {}, {}, {}

        def scale_a(g, G, t):
            if (g, G) not in eps:
                eps[g, G] = rotating("eps", [P, 4, P, 4], BF16, 3)
            species = slice(PASS * G, PASS * G + PASS)
            e_row = e_banks[G][:, t].rearrange("p (y i) -> p y i", i=4)
            nc.vector.tensor_tensor(
                out=eps[g, G][:, t].rearrange("p (y i) j -> p y j i", i=4),
                in0=a_raw[g][:, :, species].rearrange("p j (y t i) -> p t y j i", t=4, i=4)[:, t],
                in1=e_row.unsqueeze(2).to_broadcast([P, P // 4, 4, 4]),
                op=MULT,
            )

        def quantize_eps(g, G):
            eps_codes[g, G] = kept("eps_codes%d%d" % (g, G), [P, 4 * P], U32)
            eps_scales[g, G] = kept("eps_scales%d%d" % (g, G), [P, 4 * P], U8)
            quantize(eps_codes[g, G][:], eps_scales[g, G][:], eps[g, G][:].rearrange("p t m j -> p (t m j)"))

        c_op = {"tag": "c", "raw": c_raw, "values": {}, "codes": {}, "scales": {}}
        cu_op = {"tag": "cu", "raw": cu_raw, "values": {}, "codes": {}, "scales": {}}

        def interleave(op, g, h, copy):
            op["values"][g, h] = rotating("w_bf", [P, PASS, 4], BF16, 6)
            copy(
                out=op["values"][g, h][:].rearrange("p (x i) j -> p x j i", i=4),
                in_=op["raw"][g][:, :, halves[h]].rearrange("p j (x i) -> p x j i", i=4),
            )

        def quantize_columns(op, g, h):
            op["codes"][g, h] = kept("%s_codes%d%d" % (op["tag"], g, h), [P, PASS], U32)
            op["scales"][g, h] = kept("%s_scales%d%d" % (op["tag"], g, h), [P, PASS], U8)
            quantize(op["codes"][g, h][:], op["scales"][g, h][:], op["values"][g, h][:].rearrange("p z j -> p (z j)"))

        k_banks, jac, jac_codes, jac_scales = {}, {}, {}, {}

        def multiply_nv_eps(k, b, G):
            bank = k_bank()
            rows = slice(P * b, P * b + P)
            for t in range(4):
                cols = slice(P * t, P * t + P)
                for g in range(2):
                    multiply(
                        bank[:, t, :],
                        (eps_codes[g, G][:, cols], eps_scales[g, G][:, cols]),
                        (n_op["codes"][k][:, g, rows], n_op["scales"][k][:, g, rows]),
                        start=(g == 0),
                        stop=(g == 1),
                    )
            k_banks[k, b, G] = bank

        def divide_by_s(k, b, G):
            if k not in jac:
                jac[k] = rotating("jac", [P, 2, ROWS, 4], BF16, 2)
            row0 = ROWS * k + P * b
            nc.vector.tensor_tensor(
                out=jac[k][:, G, P * b : P * b + P, :],
                in0=k_banks.pop((k, b, G))[:].rearrange("p t i -> p i t"),
                in1=inv_s_row[:, row0 : row0 + P].unsqueeze(2).to_broadcast([P, P, 4]),
                op=MULT,
            )

        def quantize_jac(k):
            jac_codes[k] = rotating("jac_codes", [P, 2, ROWS], U32, 2)
            jac_scales[k] = rotating("jac_scales", [P, 2, ROWS], U8, 2)
            quantize(
                jac_codes[k][:].rearrange("p G i -> p (G i)"),
                jac_scales[k][:].rearrange("p G i -> p (G i)"),
                jac[k][:].rearrange("p G i t -> p (G i t)"),
            )

        row_banks, rounded = {}, {}

        def start_rows(k, h, b):
            row_banks[k, h, b] = row_bank([P, PASS])
            rows = slice(P * b, P * b + P)
            for g in range(2):
                multiply(
                    row_banks[k, h, b][:],
                    (l_op["codes"][k][:, g, rows], l_op["scales"][k][:, g, rows]),
                    (cu_op["codes"][g, h][:], cu_op["scales"][g, h][:]),
                    start=(g == 0),
                    stop=False,
                )

        def finish_rows(k, h, b):
            rows = slice(P * b, P * b + P)
            for G in range(2):
                multiply(
                    row_banks[k, h, b][:],
                    (jac_codes[k][:, G, rows], jac_scales[k][:, G, rows]),
                    (c_op["codes"][G, h][:], c_op["scales"][G, h][:]),
                    start=False,
                    stop=(G == 1),
                )

        def empty_rows(k, h, b, round_with, bank_first):
            bank = row_banks.pop((k, h, b))
            small = rotating("rounded", [P, PASS], BF16, 6)
            rows = rotating("rows", [P, PASS], F32, 4)
            if not bank_first:
                nc.scalar.copy(out=rows[:], in_=bank[:])
            round_with(
                out=small[:].rearrange("p (w x e) -> p w x e", w=2, e=2),
                in_=(bank if bank_first else rows)[:].rearrange("p (x w e) -> p w x e", w=2, e=2),
            )
            if bank_first:
                nc.scalar.copy(out=rows[:], in_=bank[:])
            rounded[k, h, b] = small
            row0 = ROWS * k + P * b
            nc.sync.dma_start(out=out_0[row0 : row0 + P, halves[h]], in_=rows[:])

        both = [0, 1]
        p_values = {}
        p_scales = kept("p_scales", [P, 2, N], U8)
        words_out = out_1.rearrange("g p i j -> g p (i j)").bitcast(I32)
        scales_out = out_2.bitcast(I32)

        def turn_p(k, h, blocks):
            bank = turn_bank([P, 2, len(blocks), P])
            for x, b in enumerate(blocks):
                words = rounded.pop((k, h, b))[:].bitcast(F32)
                for w in range(2):
                    nc.tensor.transpose(bank[:, w, x, :], words[:, P * w : P * w + P], identity[:])
            turned["p", k, h, blocks[0]] = bank

        def empty_p(k, h, blocks, copy):
            values = rotating("p_values", [P, P * len(blocks), 4], BF16, 3)
            lay_words(copy, values[:], turned.pop(("p", k, h, blocks[0])))
            p_values[k, h, blocks[0]] = values

        def quantize_p(k, h, blocks):
            row0 = ROWS * k + P * blocks[0]
            rows = slice(row0, row0 + P * len(blocks))
            codes = rotating("p_codes", [P, P * len(blocks)], U32, 3)
            quantize(codes[:], p_scales[:, h, rows], p_values.pop((k, h, blocks[0]))[:].rearrange("p i j -> p (i j)"))
            nc.sync.dma_start(out=words_out[h, :, rows], in_=codes[:].bitcast(I32))

        def store_scales(row0, row1):
            quads = slice(row0 // 4, row1 // 4)
            for Q in range(4):
                nc.sync.dma_start(
                    out=scales_out[:, 4 * Q : 4 * Q + 4, quads].rearrange("g r i -> r g i"),
                    in_=p_scales[32 * Q : 32 * Q + 4, :, :].bitcast(I32)[:, :, quads],
                )

        load_grouped(a_raw, a, 1, whole)
        load_grouped(cu_raw, cu, 1, whole)
        load_grouped(a_raw, a, 0, halves[0])
        load_rows(l_raw, l, 0)
        load_grouped(a_raw, a, 0, halves[1])
        load_rows(n_raw, n, 0)
        load_rows(l_raw, l, 1)
        load_rows(n_raw, n, 1)
        load_rows(l_raw, l, 3)
        load_grouped(cu_raw, cu, 0, halves[0])
        load_rows(n_raw, n, 2)
        load_c(0)

        interleave(cu_op, 1, 0, by_scalar)
        spread_e(0)
        scale_a(1, 0, 3)
        spread_e(1)
        interleave(cu_op, 1, 1, by_scalar)
        scale_a(1, 0, 0)
        spread_v()
        turn_l(0, 0)
        scale_a(1, 1, 0)
        scale_a(1, 0, 2)
        turn_l(0, 1)
        scale_a(1, 1, 2)
        scale_a(1, 0, 1)
        spread_inv_s(0)
        scale_a(0, 0, 1)
        empty_turned(l_op, 0, 0)
        scale_a(1, 1, 1)
        empty_turned(l_op, 0, 1)
        quantize_eps(1, 0)
        scale_a(0, 0, 2)
        scale_a(0, 1, 1)
        scale_a(0, 0, 0)
        scale_n(0, 1)
        spread_inv_s(1)
        scale_n(0, 0)
        scale_a(0, 0, 3)
        scale_a(1, 1, 3)
        scale_n(1, 1)
        turn_l(1, 1)
        scale_n(1, 0)
        empty_turned(l_op, 1, 1)
        turn_n(0, 0)
        scale_a(0, 1, 0)
        turn_n(0, 1)
        turn_l(3, 0)
        quantize_eps(0, 0)
        empty_turned(n_op, 0, 0)
        scale_a(0, 1, 2)
        turn_n(1, 0)
        empty_turned(n_op, 0, 1)
        load_rows(l_raw, l, 2)
        turn_n(1, 1)
        quantize_rows(n_op, 0)
        interleave(cu_op, 0, 0, by_scalar)
        scale_a(0, 1, 3)
        scale_n(2, 1)
        load_c(1)

        multiply_nv_eps(0, 0, 0)
        scale_n(2, 0)
        quantize_eps(1, 1)
        empty_turned(l_op, 3, 0)
        divide_by_s(0, 0, 0)
        empty_turned(n_op, 1, 1)
        multiply_nv_eps(0, 1, 0)
        quantize_eps(0, 1)
        divide_by_s(0, 1, 0)
        empty_turned(n_op, 1, 0)
        turn_n(2, 0)
        turn_n(2, 1)
        load_grouped(cu_raw, cu, 0, halves[1])
        turn_l(1, 0)
        interleave(c_op, 0, 0, by_scalar)
        quantize_rows(n_op, 1)
        multiply_nv_eps(0, 0, 1)
        multiply_nv_eps(0, 1, 1)
        empty_turned(n_op, 2, 0)
        turn_l(2, 0)
        load_rows(n_raw, n, 3)
        empty_turned(n_op, 2, 1)
        turn_l(2, 1)
        quantize_columns(cu_op, 0, 0)
        empty_turned(l_op, 1, 0)
        divide_by_s(0, 0, 1)
        interleave(c_op, 1, 0, by_scalar)
        divide_by_s(0, 1, 1)
        quantize_rows(l_op, 0)
        quantize_columns(cu_op, 1, 0)
        multiply_nv_eps(1, 0, 1)
        turn_l(3, 1)
        quantize_jac(0)
        multiply_nv_eps(1, 1, 0)
        divide_by_s(1, 0, 1)

        start_rows(0, 0, 1)
        quantize_columns(c_op, 0, 0)
        quantize_columns(c_op, 1, 0)
        multiply_nv_eps(1, 1, 1)
        start_rows(0, 0, 0)
        divide_by_s(1, 1, 0)
        finish_rows(0, 0, 0)
        multiply_nv_eps(1, 0, 0)
        quantize_rows(n_op, 2)
        divide_by_s(1, 1, 1)
        interleave(c_op, 0, 1, by_scalar)
        finish_rows(0, 0, 1)
        quantize_rows(l_op, 1)
        multiply_nv_eps(2, 0, 0)
        divide_by_s(1, 0, 0)
        start_rows(1, 0, 1)
        divide_by_s(2, 0, 0)
        quantize_jac(1)
        quantize_columns(cu_op, 1, 1)
        scale_n(3, 0)
        scale_n(3, 1)
        interleave(cu_op, 0, 1, by_scalar)
        quantize_columns(cu_op, 0, 1)
        interleave(c_op, 1, 1, by_vector)
        multiply_nv_eps(2, 0, 1)
        quantize_columns(c_op, 0, 1)
        multiply_nv_eps(2, 1, 0)
        quantize_columns(c_op, 1, 1)
        finish_rows(1, 0, 1)
        empty_rows(0, 0, 1, by_vector, False)
        divide_by_s(2, 0, 1)
        empty_turned(l_op, 2, 0)
        start_rows(1, 0, 0)
        empty_turned(l_op, 2, 1)
        finish_rows(1, 0, 0)
        empty_rows(0, 0, 0, by_vector, False)
        turn_n(3, 1)
        turn_n(3, 0)
        empty_rows(1, 0, 1, by_vector, False)

        start_rows(0, 1, 0)
        start_rows(1, 1, 0)
        empty_rows(1, 0, 0, by_vector, False)
        empty_turned(l_op, 3, 1)
        start_rows(1, 1, 1)
        finish_rows(0, 1, 0)
        finish_rows(1, 1, 0)
        finish_rows(1, 1, 1)
        empty_turned(n_op, 3, 0)
        multiply_nv_eps(2, 1, 1)
        empty_turned(n_op, 3, 1)
        divide_by_s(2, 1, 0)
        quantize_rows(n_op, 3)
        turn_p(0, 0, both)
        empty_rows(0, 1, 0, by_scalar, True)
        turn_p(1, 0, both)
        start_rows(0, 1, 1)
        finish_rows(0, 1, 1)
        divide_by_s(2, 1, 1)
        quantize_rows(l_op, 2)
        multiply_nv_eps(3, 0, 0)
        empty_rows(1, 1, 1, by_vector, False)
        empty_p(0, 0, both, by_scalar)
        empty_rows(1, 1, 0, by_scalar, True)
        empty_rows(0, 1, 1, by_scalar, True)
        quantize_jac(2)
        multiply_nv_eps(3, 1, 1)
        start_rows(2, 1, 0)
        divide_by_s(3, 0, 0)
        divide_by_s(3, 1, 1)
        finish_rows(2, 1, 0)
        empty_p(1, 0, both, by_scalar)
        start_rows(2, 1, 1)
        quantize_p(0, 0, both)
        finish_rows(2, 1, 1)
        empty_rows(2, 1, 0, by_vector, True)
        multiply_nv_eps(3, 1, 0)
        quantize_rows(l_op, 3)
        multiply_nv_eps(3, 0, 1)
        divide_by_s(3, 1, 0)
        turn_p(0, 1, both)
        turn_p(1, 1, both)
        empty_rows(2, 1, 1, by_scalar, True)
        divide_by_s(3, 0, 1)
        turn_p(2, 1, both)
        quantize_p(1, 0, both)

        start_rows(2, 0, 0)
        empty_p(0, 1, both, by_scalar)
        finish_rows(2, 0, 0)
        start_rows(2, 0, 1)
        empty_p(2, 1, both, by_vector)
        finish_rows(2, 0, 1)
        start_rows(3, 0, 0)
        empty_p(1, 1, both, by_scalar)
        quantize_jac(3)
        quantize_p(2, 1, both)
        finish_rows(3, 0, 0)
        quantize_p(0, 1, both)
        empty_rows(2, 0, 0, by_vector, False)
        start_rows(3, 1, 0)
        finish_rows(3, 1, 0)
        empty_rows(2, 0, 1, by_vector, True)
        quantize_p(1, 1, both)
        turn_p(2, 0, both)
        empty_rows(3, 0, 0, by_vector, True)
        turn_p(3, 0, [0])
        start_rows(3, 0, 1)
        empty_rows(3, 1, 0, by_vector, True)
        empty_p(3, 0, [0], by_scalar)
        finish_rows(3, 0, 1)
        empty_p(2, 0, both, by_vector)
        start_rows(3, 1, 1)
        quantize_p(3, 0, [0])
        quantize_p(2, 0, both)
        store_scales(0, 3 * ROWS)
        finish_rows(3, 1, 1)
        empty_rows(3, 0, 1, by_vector, True)
        turn_p(3, 1, [0])
        turn_p(3, 0, [1])
        empty_rows(3, 1, 1, by_vector, True)
        empty_p(3, 1, [0], by_scalar)
        turn_p(3, 1, [1])
        empty_p(3, 0, [1], by_vector)
        quantize_p(3, 1, [0])
        quantize_p(3, 0, [1])
        empty_p(3, 1, [1], by_scalar)
        quantize_p(3, 1, [1])
        store_scales(3 * ROWS, N)
